import numpy as np, ml_dtypes
CORES = [10,34,74,98]
N = 4
BF = ml_dtypes.bfloat16
def gentries(a):
    return np.ascontiguousarray(a.reshape(8, 16, -1).transpose(0, 2, 1)).reshape(8, -1)
def gtable(e):
    e = np.asarray(e); return np.ascontiguousarray(e.reshape(8, -1, 16).transpose(0, 2, 1)).reshape(128, -1).astype(np.int32)
NV, YM, P, LG, S, B, D0, D1 = 4096, 1024, 2048, 4, 2, 2, 800, 1000
def lst(a):
    return np.stack([gentries(b) for b in a]).astype(np.int64)
def walk(V, st, x, y, dx, dy, E, kp=None, L=None):
    logs = []
    for j in range(LG):
        for s in range(S):
            v = 64 * (y >> 4) + (x >> 4); e = E >> 6; d = np.zeros_like(E)
            for h in range(N):
                q = (h + j) % N
                a = np.take_along_axis(V[q], v[h][:, None, :], 2)
                d[h] = np.add.reduce(a * np.take_along_axis(st[q], e[h][:, None, :], 2), axis=1)
                if L is not None: L[h] += a * np.take_along_axis(kp[q], e[h][:, None, :], 2)
            E = np.maximum(E - d, 0)
            if j < LG - 1 or s < S - 1:
                t = np.where(d >= D1, 1, np.where(d >= D0, 2, 4))
                x = (x + t * dx) & 1023; y = (y + t * dy) & (YM - 1)
        logs.append(v)
    return E, logs
def verdict(E, F):
    s = np.sign(E - F)
    return np.sign(2 * s + np.add.reduce(s, axis=1, keepdims=True))
def mend(V, cor, logs, t):
    for q in range(N):
        for j in range(LG):
            h = (q - j) % N
            w = np.take_along_axis(cor[q], logs[j][h] // P * P + np.arange(P), 1)[:, None, :]
            a = np.take_along_axis(V[q], w, 2)
            np.put_along_axis(V[q], w, np.where(a > 0, np.minimum(a + t[h][:, None, :], 15), 0).astype(V.dtype), 2)
def parts(rng):
    a = {"V": rng.integers(0, 16, (N, 8, 16, NV)).astype(np.int32), "st": rng.integers(0, 16, (N, 8, 16, 1024)).astype(np.int32), "kp": np.exp2(5 * rng.random((N, 8, 16, 1024)) - 3)}
    for k, hi in (("x", 1024), ("y", YM), ("dx", 1024), ("dy", YM), ("E", 65536)): a[k] = rng.integers(0, hi, (N, 8, B, P))
    a["cor"] = np.ascontiguousarray(np.argsort(rng.random((N, 8, NV)), axis=-1))
    return a
def signs(rng):
    lean = rng.random((B - 1, N, 1, P))
    return np.where(rng.random((B - 1, N, 8, P)) < 0.25, 0, np.where(rng.random((B - 1, N, 8, P)) < lean, 1, -1))
def finish(rng, a, s=None, F=None, one=False, calm=False):
    V = a["V"].copy(); ev = (np.arange(8) % 2 == 0)[None, :, None]; out = []
    if s is None: s = signs(rng)
    for b in range(B if calm else B - 1):
        x, y, dx, dy = [a[k][:, :, b] for k in ("x", "y", "dx", "dy")]; E0 = a["E"][:, :, b]
        if calm:
            w = walk(V, a["st"], x, y, dx, dy, np.where(ev, 63, E0))[0]
            E0 = np.where(ev, np.minimum(63 - w + rng.integers(0, 4, w.shape), 63), E0); a["E"][:, :, b] = E0
            if b == B - 1: break
        E, logs = walk(V, a["st"], x, y, dx, dy, E0)
        if F is None:
            big = np.where(rng.random(E.shape) < 0.4, 1, rng.integers(1, 2000, E.shape))
            m = np.clip(E - s[b] * (1 if one else big), 0, 65535)
            if calm: m = np.where(ev, rng.integers(0, 4, E.shape), m)
        else: m = F[:, :, b]
        out.append(m); mend(V, a["cor"], logs, verdict(E, m))
    g = lambda z: np.stack([gtable(c.reshape(8, -1)) for c in z])
    r = {"slab": a["V"].reshape(N, 128, NV).astype(np.float32).astype(BF), "spow": a["st"].reshape(N, 128, 1024).astype(np.float32).astype(BF), "kap": a["kp"].reshape(N, 128, 1024).astype(np.float32).astype(BF)}
    for n, k in (("px", "x"), ("py", "y"), ("vx", "dx"), ("vy", "dy"), ("en", "E")): r[n] = g(a[k])
    r["fm"] = g(np.stack(out, axis=2)); r["cor"] = g(a["cor"])
    return r
def setup_inputs(rng):
    return finish(rng, parts(rng))
def setup_inputs_spread(rng):
    a = parts(rng); top = np.array([1, 2, 4, 8, 16, 16, 16])
    a["V"] = np.floor(rng.random((N, 8, 16, NV)) * rng.choice(top, (N, 8, 1, NV))).astype(np.int32)
    a["st"] = np.floor(rng.random((N, 8, 16, 1024)) * rng.choice(top, (N, 8, 1, 1024))).astype(np.int32)
    a["kp"] = np.exp2(rng.integers(-3, 2, (N, 8, 1, 1024))) * (1 + rng.random((N, 8, 16, 1024)))
    a["E"] = np.minimum(np.exp2(6 + 10 * rng.random((N, 8, B, P))).astype(np.int64), 65535)
    a["dx"] = np.exp2(9.99 * rng.random((N, 8, B, P))).astype(np.int64)
    return finish(rng, a)
def setup_inputs_ends(rng):
    a = parts(rng)
    def mixed(n):
        k = rng.integers(0, 4, (N, 8, 1, n))
        return np.where(k == 0, 15, np.where(k == 1, 0, 15 * rng.integers(0, 2, (N, 8, 16, n)))).astype(np.int32)
    a["V"] = mixed(NV); a["st"] = mixed(1024); a["kp"] = 4.0 * (rng.random((N, 8, 16, 1024)) < 0.4)
    for k, hi in (("x", 1023), ("y", YM - 1), ("dx", 1023), ("dy", YM - 1)): a[k] = hi * rng.integers(0, 2, (N, 8, B, P))
    a["E"] = 65535 * (rng.random((N, 8, B, P)) < 0.7).astype(np.int64)
    a["st"][:, 7] = np.where(rng.random((N, 1, 1024)) < 0.7, 15, a["st"][:, 7])
    a["st"][:, 7, :, 1023] = 15
    a["st"][:, 3, :, 1023] = 0
    for g in (3, 7):
        a["kp"][:, g, :, 1023] = 4.0
        for v in (0, 63, NV - 64, NV - 1): a["V"][:, g, :, v] = 15
        for p in (0, 1, P - 2, P - 1):
            a["x"][:, g, :, p] = 1023; a["y"][:, g, :, p] = YM - 1; a["dx"][:, g, :, p] = 0; a["dy"][:, g, :, p] = 0; a["E"][:, g, :, p] = 65535
    z = np.zeros(NV, np.int64); z[0::2] = np.arange(NV // 2); z[1::2] = NV - 1 - np.arange(NV // 2)
    for q in range(N):
        for g in range(8): a["cor"][q, g] = np.roll(z, int(rng.integers(0, NV)))
    return finish(rng, a, F=65535 * rng.integers(0, 2, (N, 8, B - 1, P)))
def setup_inputs_corners(rng):
    a = parts(rng); kd = (rng.permutation(8)[None, :] + np.arange(N)[:, None]) % 8
    first = P * np.arange(NV // P); edge = np.concatenate([first, first + P - 1])
    for q in range(N):
        for g in range(8):
            c = int(kd[q, g])
            if c in (0, 1, 2): a["V"][q, g] = (0, 15, 1)[c]
            if c in (3, 4): a["V"][q, g] = rng.integers(0, 2, (16, NV)) + (0 if c == 3 else 14)
            if c in (0, 1):
                a["x"][q, g] = 1023 * c; a["y"][q, g] = (YM - 1) * c; a["dx"][q, g] = 0; a["dy"][q, g] = 0
            if c == 2:
                a["x"][q, g] = 1023 - rng.integers(0, 2, (B, P)); a["y"][q, g] = YM - 1 - rng.integers(0, 2, (B, P)); a["dx"][q, g] = 1; a["dy"][q, g] = 1
            if c == 3:
                v = rng.choice(edge, (B, P))
                a["x"][q, g] = 16 * (v & 63) + rng.integers(0, 16, (B, P)); a["y"][q, g] = 16 * (v >> 6) + rng.integers(0, 16, (B, P)); a["dx"][q, g] = 0; a["dy"][q, g] = 0
            if c == 4: a["dx"][q, g] = 1023; a["dy"][q, g] = YM - 1
            if c == 5: a["E"][q, g] = rng.choice(np.array([0, 1, 63, 64, 65535]), (B, P))
            if c == 6: a["E"][q, g] = rng.integers(0, 3601, (B, P))
            if c == 1: a["cor"][q, g] = np.arange(NV)
            if c == 2: a["cor"][q, g] = np.arange(NV)[::-1]
    t = np.array([[1] * 8, [-1] * 8, [1] * 7 + [0], [-1] * 7 + [0], [1] * 7 + [-1], [-1] * 7 + [1], [1, -1] * 4, [1] + [0] * 7, [-1] + [0] * 7, [0] * 8,
                  [1, -1, -1, -1, 0, 0, 0, 0], [1, -1, -1, -1, -1, 0, 0, 0], [-1, 1, 1, 1, 0, 0, 0, 0], [-1, 1, 1, 1, 1, 0, 0, 0]])
    i = rng.integers(0, 14, (B - 1, N, 1, P)); o = rng.integers(0, 8, (B - 1, N, 1, P))
    return finish(rng, a, s=t[i, (np.arange(8)[None, None, :, None] + o) % 8])
def setup_inputs_ties(rng):
    a = parts(rng); t = rng.choice(np.array([D0 - 1, D0, D1 - 1, D1]), (N, 8, 1024)); t[..., D0 >> 6] = D0
    m = t // 15; k = np.argsort(rng.random((N, 8, 15, 1024)), axis=2)
    st = np.concatenate([(m // 15)[:, :, None] + (k < (m % 15)[:, :, None]), (t - 15 * m)[:, :, None]], axis=2)
    u = np.array([15] * 15 + [1]); pm = np.argsort(rng.random((N, 8, 16)), axis=-1)
    st = np.take_along_axis(st, pm[..., None], 2); v = np.broadcast_to(u[pm][..., None], (N, 8, 16, NV))
    a["V"][:, ::2] = v[:, ::2]; a["st"][:, ::2] = st[:, ::2]
    p = np.arange(P) % 4; E = a["E"]
    E = np.where(p == 0, D0 + rng.integers(-1, 2, E.shape), np.where(p == 1, 64 * rng.integers(1, 1024, E.shape) - rng.integers(0, 2, E.shape), E))
    a["E"][:, ::2] = E[:, ::2]
    return finish(rng, a, one=True)
def setup_inputs_calm(rng):
    a = parts(rng)
    v = np.where(rng.random((N, 8, 16, NV)) < 0.25, rng.integers(1, 4, (N, 8, 16, NV)), 0); a["V"][:, ::2] = v[:, ::2]
    k = np.argsort(rng.random((N, 8, 16)), axis=-1) < 2
    a["st"][:, ::2, :, 0] = k[:, ::2]
    return finish(rng, a, calm=True)
def check_ranges(d):
    bad = []
    for k, lo, hi in (("slab", 0, 15), ("spow", 0, 15), ("kap", 0, 4), ("px", 0, 1023), ("py", 0, YM - 1), ("vx", 0, 1023), ("vy", 0, YM - 1), ("en", 0, 65535), ("fm", 0, 65535), ("cor", 0, NV - 1)):
        a = np.asarray(d[k]).astype(np.float64)
        if not (np.min(a) >= lo and np.max(a) <= hi): bad.append("range of " + k)
        elif k in ("slab", "spow") and np.any(a != np.floor(a)): bad.append("whole numbers of " + k)
    if np.any(np.sort(lst(np.asarray(d["cor"])), axis=-1) != np.arange(NV)): bad.append("each voxel once in cor")
    return bad
def reference(slab, spow, kap, px, py, vx, vy, en, fm, cor):
    V = slab.astype(np.float32).astype(np.int32).reshape(N, 8, 16, NV); st = spow.astype(np.float32).astype(np.int32).reshape(N, 8, 16, 1024)
    kp = kap.astype(np.float64).reshape(N, 8, 16, 1024); x, y, dx, dy, E0 = [lst(a).reshape(N, 8, B, P) for a in (px, py, vx, vy, en)]
    F = lst(fm).reshape(N, 8, B - 1, P); cl = lst(cor); L = np.zeros((N, 8, 16, P)); E = np.zeros((N, 8, B, P), np.int64)
    for b in range(B):
        E[:, :, b], logs = walk(V, st, x[:, :, b], y[:, :, b], dx[:, :, b], dy[:, :, b], E0[:, :, b], kp, L)
        if b < B - 1: mend(V, cl, logs, verdict(E[:, :, b], F[:, :, b]))
    ye = np.stack([gtable((E[r] & 1023).reshape(8, B * P)) for r in range(N)])
    return {"yl": np.exp(L * -0.0078125).reshape(N, 128, P).astype(np.float32), "ye": ye.astype(np.float32)}

def check_inputs(d):
    bad = list(check_ranges(d))
    if not bad:
        for name, y in reference(**d).items():
            for q in range(N):
                v = np.abs(np.asarray(y[q], np.float64))
                if v.max() > 5 * np.sqrt(np.mean(v * v)): bad.append('%s of rank %d is uneven' % (name, q))
    return bad

@@ -1,0 +1,570 @@
+from concourse.bass import DstId, RemoteDMATransfer
+from concourse.mybir import dt, AluOpType, AxisListType, ActivationFunctionType
+
+N = 4
+SIM_CORES = 112
+BF, F32, I32, U16 = "bfloat16", "float32", "int32", "uint16"
+
+SCRATCH = {}
+for _j in range(N):
+    SCRATCH["tab%d" % _j] = ("sbuf", [128, 6144], BF)
+    SCRATCH["slb%d" % _j] = ("sbuf", [128, 4096], BF)
+    SCRATCH["uin%d" % _j] = ("sbuf", [128, 256], BF)
+    SCRATCH["uout%d" % _j] = ("sbuf", [128, 256], BF)
+for _n in ("lx", "ly", "ldx", "ldy", "le", "lcor", "y4", "dy4", "ta", "tb", "tc", "td", "invi"):
+    SCRATCH[_n] = ("sbuf", [128, 256], I32)
+for _n in ("lf", "ci", "ef", "lo", "c1", "ee", "vxb", "vyb", "vb", "df"):
+    SCRATCH[_n] = ("sbuf", [128, 128], I32)
+for _n in ("cor16", "coro16", "inv16"):
+    SCRATCH[_n] = ("sbuf", [128, 256], U16)
+for _n in ("v16", "e16"):
+    SCRATCH[_n] = ("sbuf", [128, 2048], U16)
+for _n in ("idb", "id32", "idn", "c0", "cm", "sb"):
+    SCRATCH[_n] = ("sbuf", [128, 128], BF)
+for _h in range(2):
+    SCRATCH["am%d" % _h] = ("sbuf", [128, 1024], BF)
+    SCRATCH["pa%d" % _h] = ("sbuf", [128, 1024], BF)
+    SCRATCH["pb%d" % _h] = ("sbuf", [128, 1024], F32)
+    SCRATCH["gb%d" % _h] = ("sbuf", [128, 256], BF)
+    SCRATCH["mb%d" % _h] = ("sbuf", [128, 256], BF)
+for _b in range(8):
+    SCRATCH["ps%d" % _b] = ("psum", [128, 512], F32)
+SCRATCH.update({
+    "ones": ("sbuf", [128, 128], F32), "idf": ("sbuf", [128, 128], F32),
+    "b8a": ("sbuf", [128, 8], F32), "b8b": ("sbuf", [128, 8], F32),
+    "qq": ("sbuf", [128, 144], BF), "wp": ("sbuf", [128, 2048], BF), "rst": ("sbuf", [128, 512], F32),
+    "iot": ("sbuf", [128, 4096], F32), "invr": ("sbuf", [128, 4096], F32), "invl": ("sbuf", [128, 256], F32),
+    "acor": ("sbuf", [128, 4096], BF), "ac15": ("sbuf", [128, 4096], BF), "fn": ("sbuf", [128, 4096], BF),
+    "mk": ("sbuf", [128, 1024], BF), "scm": ("sbuf", [128, 1024], BF), "scz": ("sbuf", [128, 1024], BF),
+    "tt": ("sbuf", [128, 256], BF), "ylb": ("sbuf", [128, 2048], F32), "yeb": ("sbuf", [128, 256], F32),
+})
+
+_HALF = ["pa", "pb", "c1", "c2", "en", "m", "e", "mx", "my", "e16", "x", "y", "vx", "vy", "v", "v16", "ka", "kb",
+         "aa", "ab", "d", "l", "uz", "g", "mm", "xx", "f", "n", "sm", "sz", "tc", "ex", "uu"]
+SEMAPHORES = ([n + str(h) for n in _HALF for h in range(2)]
+              + ["ld%d" % p for p in range(8)] + ["li%d" % p for p in range(7)] + ["pm%d" % p for p in range(8)]
+              + ["va", "vb", "vc", "vd", "ve", "vf", "ga", "gb", "gc0", "gd", "ge", "gi0", "gi1", "gi2", "gi3",
+                 "sct", "aco", "a15", "ivd", "st", "ls", "ua"]
+              + ["tb%d%d" % (b, j) for b in range(2) for j in (1, 2, 3)]
+              + ["ha%d" % i for i in range(4)] + ["rl%d" % i for i in range(8)])
+
+PIECE = (768, 512)
+
+
+def ways(T, topo):
+    cores = T.cores
+    senders = []
+    for r in range(N):
+        c = cores[r]
+        able = [k for k in topo.cores_of(c) if k != c and all(topo.may_write(k, d) for d in cores if d != c)]
+        near = [k for k in able if topo.die(k) == topo.die(c)]
+        far = [k for k in able if topo.die(k) != topo.die(c)]
+        senders.append([far[1], near[0], far[0], c])
+
+    def relay(r, q, j):
+        if q >= 2:
+            return None
+        d = cores[(r - j) % N]
+        s = senders[r][q]
+        able = [k for k in range(SIM_CORES) if topo.mates(topo.chip(k), topo.chip(d)) and topo.die(k) == topo.die(s)
+                and topo.may_write(k, d) and topo.may_write(s, k)]
+        return able[(j - 1) % len(able)]
+    return senders, relay
+
+
+def parts(b, q, j):
+    w = PIECE[b]
+    if j == 1:
+        return [(2 * q * w, (2 * q + 1) * w), ((2 * q + 1) * w, (2 * q + 2) * w)]
+    return [(2 * q * w, (2 * q + 2) * w)]
+
+
+def relay_sem(b, j, i):
+    return "rl%d" % (4 * b + (i if j == 1 else j))
+
+
+def send(g, T, topo, src, dst, out, in_, sem, mask=None):
+    rid, pid = topo.addr(dst)[:2]
+    m = topo.mask(src, dst) if mask is None else mask
+    g.remote_dma(out, in_, T.sem[sem], T.sem.ls, pid, rid, m)
+    return bin(m).count("1")
+
+
+def send_part(g, T, topo, relay, r, src, b, q, j, i):
+    name = ("tab%d", "slb%d")[b]
+    lo, hi = parts(b, q, j)[i]
+    via = relay(r, q, j)
+    if via is None:
+        return send(g, T, topo, src, T.cores[(r - j) % N], T[name % j][:, lo:hi], T[name % 0][:, lo:hi], "tb%d%d" % (b, j))
+    return send(g, T, topo, src, via, T[name % j][:, lo:hi], T[name % 0][:, lo:hi], relay_sem(b, j, i))
+
+
+def spare_mask(topo, src, near, far):
+    off = topo.engines(src, far)
+    return sum(1 << e for e in topo.engines(src, near) if e not in off)
+
+
+def helper_program(g, core, T, topo):
+    senders, relay = ways(T, topo)
+    sent = 0
+    for r in range(N):
+        for q in range(3):
+            if senders[r][q] != core:
+                continue
+            c = T.cores[r]
+            k = bin(spare_mask(topo, c, core, T.cores[(r + 1) % N])).count("1")
+            for b in range(2):
+                for j in (1, 2, 3):
+                    for i in range(len(parts(b, q, j))):
+                        if j == 1:
+                            g.wait_ge(T.sem["ha%d" % (2 * b + i)], k)
+                        sent += send_part(g, T, topo, relay, r, core, b, q, j, i)
+    for b in range(2):
+        for j in (1, 2, 3):
+            for r in range(N):
+                for q in range(2):
+                    if relay(r, q, j) != core:
+                        continue
+                    d = T.cores[(r - j) % N]
+                    for i, (lo, hi) in enumerate(parts(b, q, j)):
+                        g.wait_ge(T.sem[relay_sem(b, j, i)], len(topo.engines(senders[r][q], core)))
+                        buf = T[("tab%d", "slb%d")[b] % j][:, lo:hi]
+                        sent += send(g, T, topo, core, d, buf, buf, "tb%d%d" % (b, j))
+    if sent:
+        g.wait_ge(T.sem.ls, sent)
+
+
+def rank_program(g, core, T, topo):
+    rank = T.rank_of(core)
+    if rank is None:
+        helper_program(g, core, T, topo)
+        return
+    A = AluOpType
+    AF = ActivationFunctionType
+    V, S, PE = g.vector, g.scalar, g.tensor
+    Q = {"g": g, "v": V, "s": S, "t": PE, "y": g.sync}
+    senders, relay = ways(T, topo)
+    ps = [T["ps%d" % b] for b in range(8)]
+
+    know = {q: {} for q in Q}
+    cnt, lastw, readers, lastsem, banks = {}, {}, {}, {}, {}
+    tick = [0]
+    sent = [0]
+
+    def need(q, toks):
+        for t in sorted(toks, key=lambda t: -t["i"]):
+            if know[q].get(t["s"], 0) < t["n"]:
+                Q[q].wait_ge(T.sem[t["s"]], t["n"])
+                for s, n in t["k"].items():
+                    if know[q].get(s, 0) < n:
+                        know[q][s] = n
+
+    def deps(q, reads, writes, bank):
+        d = [lastw[k] for k in list(reads) + list(writes) if k in lastw]
+        for k in writes:
+            d += readers.get(k, [])
+        for b in bank:
+            for e, ts in banks.get(b, {}).items():
+                if e != q:
+                    d += ts
+        return d
+
+    def op(q, sem, call, reads=(), writes=(), bank=(), inc=1, tok=None):
+        d = deps(q, reads, writes, bank)
+        if tok is None and sem in lastsem:
+            d.append(lastsem[sem])
+        need(q, [t for t in d if t is not tok])
+        call().then_inc(T.sem[sem], inc)
+        cnt[sem] = cnt.get(sem, 0) + inc
+        tick[0] += 1
+        if tok is None:
+            tok = {"s": sem}
+        tok["n"] = cnt[sem]
+        tok["i"] = tick[0]
+        tok["k"] = dict(know[q])
+        tok["k"][sem] = cnt[sem]
+        lastsem[sem] = tok
+        for k in writes:
+            lastw[k] = tok
+            readers[k] = []
+        for k in reads:
+            readers.setdefault(k, []).append(tok)
+        for b in bank:
+            banks[b] = {q: banks.get(b, {}).get(q, []) + [tok]}
+        return tok
+
+    def arrival(sem, n, key):
+        tick[0] += 1
+        cnt[sem] = n
+        lastw[key] = {"s": sem, "n": n, "i": tick[0], "k": {sem: n}}
+
+    def ts(sem, out, in0, s1, op0, s2=None, op1=None, **kw):
+        if op1 is None:
+            return op("v", sem, lambda: V.tensor_scalar(out, in0, s1, None, op0), **kw)
+        return op("v", sem, lambda: V.tensor_scalar(out, in0, s1, s2, op0, op1), **kw)
+
+    def tt(sem, out, in0, in1, o, **kw):
+        return op("v", sem, lambda: V.tensor_tensor(out, in0, in1, o), **kw)
+
+    def cp(sem, out, in_, **kw):
+        return op("v", sem, lambda: V.tensor_copy(out, in_), **kw)
+
+    def mms(sem, group, **kw):
+        def call():
+            for a in group[:-1]:
+                PE.matmul(*a)
+            return PE.matmul(*group[-1])
+        return op("t", sem, call, **kw)
+
+    def load(q, sem, out, in_, key, tok=None):
+        return op(q, sem, lambda: Q[q].dma_start(out, in_), writes=[key], inc=16, tok=tok)
+
+    load("s", "li0", T.lx[:], T.px[:], "lx")
+    load("s", "li1", T.ly[:], T.py[:], "ly")
+    load("s", "li2", T.le[:], T.en[:], "le")
+    load("s", "li3", T.lcor[:], T.cor[:], "lcor")
+    srcs = ((0, 4096, T.slab), (4096, 5120, T.spow), (5120, 6144, T.kap))
+    for p in range(8):
+        tok = None
+        for a, z, t in srcs:
+            lo, hi = max(a, 768 * p), min(z, 768 * p + 768)
+            if lo < hi:
+                tok = load("y", "ld%d" % p, T.tab0[:, lo:hi], t[:, lo - a:hi - a], "tab0.%d.%d" % (p, a), tok)
+    load("y", "li4", T.ldx[:], T.vx[:], "ldx")
+    load("y", "li5", T.ldy[:], T.vy[:], "ldy")
+    load("y", "li6", T.lf[:], T.fm[:], "lf")
+    own = {0: ["tab0.%d.0" % p for p in range(6)], 1: ["tab0.5.4096", "tab0.6.4096"], 2: ["tab0.6.5120", "tab0.7.5120"]}
+    for j in (1, 2, 3):
+        for b in range(2):
+            n = 0
+            for q in range(4):
+                r = (rank + j) % N
+                last = relay(r, q, j)
+                last = senders[r][q] if last is None else last
+                n += len(parts(b, q, j)) * len(topo.engines(last, core))
+            arrival("tb%d%d" % (b, j), n, "in%d%d" % (b, j))
+    arrival("ua", sum(len(topo.engines(T.cores[(rank - j) % N], core)) for j in (1, 2, 3)), "uin")
+
+    op("v", "va", lambda: V.memset(T.ones[:], 1.0), writes=["ones"])
+    op("v", "vb", lambda: V.memset(T.qq[:], 0.0), writes=["qq"])
+    op("v", "vc", lambda: V.memset(T.rst[:], 1.0), writes=["rst"])
+    op("g", "gi0", lambda: g.iota(T.iot[:, 0:1024], [[1, 64], [256, 16]], 512, 0, allow_small_or_imprecise_dtypes=True), writes=["iot0"])
+    op("g", "ga", lambda: g.affine_select(T.b8a[:], T.ones[:, 0:8], [[-16, 8]], A.is_ge, 0.0, 0, 1), reads=["ones"], writes=["b8a"])
+    op("g", "gb", lambda: g.affine_select(T.idf[:], T.ones[:], [[-1, 128]], A.is_equal, 0.0, 0, 1), reads=["ones"], writes=["idf"])
+    op("g", "gc0", lambda: g.affine_select(T.b8b[:], T.b8a[:], [[16, 8]], A.is_ge, 0.0, 15, -1), reads=["b8a"], writes=["b8b"])
+    op("g", "gd", lambda: g.iota(T.ci[:], [[0, 8], [-1, 16]], 128, 1), writes=["ci"])
+    op("v", "vd", lambda: V.memset(T.rst[:, 0:512:4], 0.0), writes=["rst"])
+    ts("va", T.ta[:], T.lx[:], 4, A.arith_shift_right, reads=["lx"], writes=["ta"])
+    ts("vb", T.y4[:], T.ly[:], 4.0, A.mult, reads=["ly"], writes=["y4"])
+    ts("vc", T.tc[:], T.le[:], 6, A.arith_shift_right, reads=["le"], writes=["tc"])
+    ts("vd", T.tb[:], T.y4[:], 0xFC0, A.bitwise_and, reads=["y4"], writes=["tb"])
+    for b in range(2):
+        cp("ve", T.e16[:, 1024 * b:1024 * b + 128], T.tc[:, 128 * b:128 * b + 128], reads=["tc"], writes=["e16.%d" % (16 * b), "e16.%d" % (16 * b + 1)])
+        if b == 0:
+            tt("va", T.td[:], T.ta[:], T.tb[:], A.add, reads=["ta", "tb"], writes=["td"])
+    for b in range(2):
+        cp("vf", T.v16[:, 1024 * b:1024 * b + 128], T.td[:, 128 * b:128 * b + 128], reads=["td"], writes=["v16.%d" % (16 * b), "v16.%d" % (16 * b + 1)])
+        if b == 0:
+            ts("vb", T.ta[:], T.lcor[:], 15, A.bitwise_and, reads=["lcor"], writes=["ta"])
+    ts("vc", T.tb[:], T.lcor[:], 4, A.arith_shift_right, reads=["lcor"], writes=["tb"])
+    ts("vd", T.tc[:], T.ta[:], 256.0, A.mult, reads=["ta"], writes=["tc"])
+    cp("va", T.qq[:, 15:128:16], T.b8b[:], reads=["b8b"], writes=["qq"])
+    tt("vb", T.td[:], T.tc[:], T.tb[:], A.add, reads=["tc", "tb"], writes=["td"])
+    cp("vc", T.cor16[:], T.lcor[:], reads=["lcor"], writes=["cor16"])
+    cp("vd", T.coro16[:], T.td[:], reads=["td"], writes=["coro16"])
+    ts("ve", T.ci[:], T.ci[:], 15, A.bitwise_and, reads=["ci"], writes=["ci"])
+    ts("vf", T.cm[:], T.idf[:], 2.0, A.mult, reads=["idf"], writes=["cm"])
+    ts("va", T.c0[:], T.ci[:], 0.0, A.is_equal, reads=["ci"], writes=["c0"])
+    cp("vb", T.idb[:], T.idf[:], reads=["idf"], writes=["idb"])
+    ts("vc", T.id32[:], T.idf[:], 32.0, A.mult, reads=["idf"], writes=["id32"])
+    ts("vd", T.idn[:], T.idf[:], -1.0, A.mult, reads=["idf"], writes=["idn"])
+    tt("ve", T.cm[:], T.cm[:], T.c0[:], A.add, reads=["cm", "c0"], writes=["cm"])
+
+    spare = spare_mask(topo, core, senders[rank][0], T.cores[(rank + 1) % N])
+
+    def hand_out(b, order, keys):
+        name = ("tab0", "slb0")[b]
+        w = PIECE[b]
+        for p in order:
+            need("g", deps("g", keys(p), (), ()))
+            if p < 6:
+                buf = T[name][:, p * w:(p + 1) * w]
+                sent[0] += send(g, T, topo, core, senders[rank][p // 2], buf, buf, "ha%d" % (2 * b + p % 2), spare)
+            else:
+                sent[0] += send_part(g, T, topo, relay, rank, core, b, 3, 1, p - 6)
+        for j in (2, 3):
+            sent[0] += send_part(g, T, topo, relay, rank, core, b, 3, j, 0)
+
+    hand_out(0, range(8), lambda p: ["tab0.%d.%d" % (p, a) for a in (0, 4096, 5120)])
+    for i in (1, 2, 3):
+        op("g", "gi%d" % i, lambda: g.iota(T.iot[:, 1024 * i:1024 * i + 1024], [[1, 64], [256, 16]], 512 + 64 * i, 0, allow_small_or_imprecise_dtypes=True), writes=["iot%d" % i])
+    op("g", "ge", lambda: g.iota(T.wp[:], [[0, 2048]], 1, 0, allow_small_or_imprecise_dtypes=True), writes=["wp"])
+    op("g", "ga", lambda: g.affine_select(T.wp[:], T.wp[:], [[-1, 16], [-16, 8], [0, 16]], A.is_equal, 0.0, 0, 1), reads=["wp"], writes=["wp"])
+
+    def scatter(i):
+        op("s", "sct", lambda: S.activation(T.invr[:, 0:4096].indirect(T.coro16[:, 16 * i:16 * i + 16]), T.iot[:, 256 * i:256 * i + 256], AF.Silu),
+           reads=["coro16", "iot%d" % (i // 4)], writes=["invr"])
+
+    grp = {}
+
+    def side(u):
+        if 1 <= u <= 14:
+            scatter(u + 1)
+        if 1 <= u <= 8:
+            i = u - 1
+            grp["aco"] = op("s", "aco", lambda: S.activation(T.acor[:, 512 * i:512 * i + 512], T.tab0[:, 0:4096].indirect(T.cor16[:, 32 * i:32 * i + 32]), AF.Copy),
+                            reads=["cor16"] + own[0], writes=["acor"], tok=grp.get("aco"))
+        if 10 <= u <= 13:
+            i = u - 10
+            grp["a15"] = op("s", "a15", lambda: S.activation(T.ac15[:, 1024 * i:1024 * i + 1024], T.acor[:, 1024 * i:1024 * i + 1024], AF.Identity, bias=-15.0),
+                            reads=["acor"], writes=["ac15"], tok=grp.get("a15"))
+        if u == 14:
+            tok = None
+            for k in range(8):
+                tok = op("y", "ivd", lambda: g.sync.dma_start(T.invl[16 * k:16 * k + 16, :], T.invr[16 * k:16 * k + 1, :]),
+                         reads=["invr"], writes=["invl"], inc=16, tok=tok)
+
+    def tables(u):
+        b, j = u // 16, (u % 16) // 4
+        tab = T["tab%d" % j]
+        slab = tab[:, 0:4096] if b == 0 else T["slb%d" % j][:, 0:4096]
+        if j == 0:
+            keys = [own[0] if b == 0 else ["slb0.%d" % p for p in range(8)], own[1], own[2]]
+        else:
+            keys = [["in%d%d" % (b, j)], ["in0%d" % j], ["in0%d" % j]]
+        return slab, tab[:, 4096:5120], tab[:, 5120:6144], keys
+
+    def amounts(u):
+        h = u % 2
+        slab, _, _, keys = tables(u)
+        for i in range(2):
+            op("s", ("aa", "ab")[i] + str(h),
+               lambda: S.activation(T["am%d" % h][:, 512 * i:512 * i + 512], slab.indirect(T.v16[:, 64 * u + 32 * i:64 * u + 32 * i + 32]), AF.Copy),
+               reads=keys[0] + ["v16.%d" % u], writes=["am%d.%d" % (h, i)])
+        side(u)
+
+    def product(u, which, lo, hi):
+        h = u % 2
+        t = tables(u)
+        name = ("pa", "pb")[which - 1] + str(h)
+        key = (name, u)
+        grp[key] = tt(name, T[name][:, lo:hi], t[which].indirect(T.e16[:, 64 * u + lo // 16:64 * u + hi // 16]), T["am%d" % h][:, lo:hi], A.mult,
+                      reads=t[3][which] + ["e16.%d" % u] + ["am%d.%d" % (h, i) for i in range(lo // 512, (hi - 1) // 512 + 1)],
+                      writes=[name], tok=grp.get(key))
+
+    def loss(u):
+        h = u % 2
+        mms("d%d" % h, [(ps[4 + h][:, 0:64], T.qq[:, 15 - r:143 - r], T["pa%d" % h][:, r:1024:16], r == 0, r == 15) for r in range(16)],
+            reads=["qq", "pa%d" % h], writes=["d%d" % h], bank=[4 + h])
+
+    def addl(u):
+        h = u % 2
+        tok = None
+        for i in range(2):
+            tok = op("t", "l%d" % h, lambda: PE.matmul(ps[2 * h + i][:], T.idf[:], T["pb%d" % h][:, 512 * i:512 * i + 512], u < 2, u >= 30),
+                     reads=["idf", "pb%d" % h], writes=["L%d" % (2 * h + i)], bank=[2 * h + i], tok=tok)
+
+    def level(u, k):
+        if u < 0:
+            return
+        h, b = u % 2, u // 16
+        H = str(h)
+        c = slice(64 * h, 64 * h + 64)
+        cb = slice(128 * b + 64 * h, 128 * b + 64 * h + 64)
+        P = ps[4 + h]
+        bk = [4 + h]
+        d, c2, m, mx, my = P[:, 0:64], P[:, 64:128], P[:, 128:192], P[:, 192:256], P[:, 256:320]
+        kE, kx, ky = "E%d%d" % (b, h), "x%d%d" % (b, h), "y%d%d" % (b, h)
+        last = u % 16 >= 14
+        if k == 1:
+            if u in (14, 15):
+                tt("c1" + H, T.df[:, c], T.ef[:, c], d, A.subtract, reads=["ef" + H, "d" + H], writes=["df" + H], bank=bk)
+            if not last:
+                ts("c1" + H, T.c1[:, c], d, 800.0, A.is_lt, 2.0, A.mult, reads=["d" + H], writes=["c1" + H], bank=bk)
+                ts("c2" + H, c2, d, 1000.0, A.is_lt, 1.0, A.add, reads=["d" + H], writes=["c2" + H], bank=bk)
+            tt("en" + H, T.le[:, cb], T.le[:, cb], d, A.subtract, reads=["le", kE, "d" + H], writes=[kE], bank=bk)
+            return
+        if u in (14, 15):
+            Z = ps[6 + h]
+            if k == 2:
+                ts("m" + H, T.df[:, c], T.df[:, c], -1.0, A.max, 1.0, A.min, reads=["df" + H], writes=["df" + H])
+            if k == 3:
+                tt("mx" + H, T.sb[:, c], T.df[:, c], T.lo[:, c], A.max, reads=["df" + H, "lo"], writes=["sb" + H])
+                mms("uz" + H, [(Z[:, 0:64], T.cm[:], T.sb[:, c], True, True)], reads=["cm", "sb" + H], writes=["z" + H], bank=[6 + h])
+            if k == 4:
+                ts("x" + H, Z[:, 64:128], Z[:, 0:64], -1.0, A.max, 1.0, A.min, reads=["z" + H], writes=["t" + H], bank=[6 + h])
+            if k >= 5:
+                for j in {5: (1,), 6: (2,), 7: (3,), 8: (0,)}[k]:
+                    out = T["uout%d" % j] if j else T.uin0
+                    tok = None
+                    for kk in range(2):
+                        o = 128 * kk + 64 * h
+                        tok = tt(("vx", "vy", "v", "v16")[j] + H, out[:, o:o + 64], T.mk[:, 256 * j + o:256 * j + o + 64], Z[:, 64:128], A.mult,
+                                 reads=["t" + H, "mk%d%d%d" % (j, h, kk)], writes=["u%d%d" % (j, h)], bank=[6 + h], tok=tok)
+            return
+        if last:
+            return
+        if k == 2:
+            tt("m" + H, m, T.c1[:, c], c2, A.add, reads=["c1" + H, "c2" + H], writes=["m" + H], bank=bk)
+            ts("e" + H, T.ee[:, c], T.le[:, cb], 6, A.arith_shift_right, reads=[kE], writes=["ee" + H])
+        if k == 3:
+            tt("mx" + H, mx, T.ldx[:, cb], m, A.mult, reads=["ldx", "m" + H], writes=["mx" + H], bank=bk)
+            tt("my" + H, my, T.dy4[:, cb], m, A.mult, reads=["dy4", "m" + H], writes=["my" + H], bank=bk)
+            cp("e16" + H, T.e16[:, 64 * (u + 2):64 * (u + 2) + 64], T.ee[:, c], reads=["ee" + H], writes=["e16.%d" % (u + 2)])
+            if u in (12, 13):
+                tt("c2" + H, T.ef[:, c], T.le[:, cb], T.lf[:, c], A.subtract, reads=[kE, "lf"], writes=["ef" + H])
+        if k == 4:
+            tt("x" + H, T.lx[:, cb], T.lx[:, cb], mx, A.add, reads=["lx", kx, "mx" + H], writes=[kx], bank=bk)
+            tt("y" + H, T.y4[:, cb], T.y4[:, cb], my, A.add, reads=["y4", ky, "my" + H], writes=[ky], bank=bk)
+        if k == 5:
+            ts("vx" + H, T.vxb[:, c], T.lx[:, cb], 1023, A.bitwise_and, 4, A.arith_shift_right, reads=[kx], writes=["vxb" + H])
+            ts("vy" + H, T.vyb[:, c], T.y4[:, cb], 0xFC0, A.bitwise_and, reads=[ky], writes=["vyb" + H])
+        if k == 6:
+            tt("v" + H, T.vb[:, c], T.vxb[:, c], T.vyb[:, c], A.add, reads=["vxb" + H, "vyb" + H], writes=["vb" + H])
+        if k == 7:
+            cp("v16" + H, T.v16[:, 64 * (u + 2):64 * (u + 2) + 64], T.vb[:, c], reads=["vb" + H], writes=["v16.%d" % (u + 2)])
+
+    def bands(u):
+        if u < 0 or u >= 14 or (u // 2) % 2:
+            return
+        h, j = u % 2, u // 4
+        for kk in range(2):
+            o = 256 * j + 128 * kk + 64 * h
+            ts(("ka", "kb")[kk] + str(h), T.mk[:, o:o + 64], T.vb[:, 64 * h:64 * h + 64], 2048.0, (A.is_lt, A.is_ge)[kk],
+               reads=["vb%d" % h], writes=["mk%d%d%d" % (j, h, kk)])
+
+    def first_part(u):
+        prev = u - 1 if u % 16 else -1
+        for i in range(4):
+            product(u, 1, 256 * i, 256 * i + 256)
+            if i == 3:
+                loss(u)
+            level(prev, 4 + i)
+        if prev >= 0:
+            if u % 16 < 15:
+                amounts(u + 1)
+            bands(prev)
+
+    def second_part(u):
+        for k, (lo, hi) in enumerate(((0, 640), (640, 832), (832, 1024))):
+            product(u, 2, lo, hi)
+            level(u, 1 + k)
+
+    def energies(b, c, tag):
+        keys = ["E%d%d" % (b, h) for h in range(2)]
+        ts("va", T.ta[:, c], T.le[:, c], 0.0, A.max, reads=keys, writes=["ta"])
+        yield
+        ts("vb", T.tb[:, c], T.ta[:, c], 1023, A.bitwise_and, reads=["ta"], writes=["tb"])
+        yield
+        cp("vc", T.yeb[:, c], T.tb[:, c], reads=["tb"], writes=["yeb" + tag])
+        yield
+
+    scatter(0)
+    scatter(1)
+    amounts(0)
+    amounts(1)
+    for u in range(15):
+        first_part(u)
+        if u == 0:
+            ts("va", T.dy4[:], T.ldy[:], 4.0, A.mult, reads=["ldy"], writes=["dy4"])
+        if u == 1:
+            ts("vb", T.lo[:], T.lf[:], 0.0, A.is_gt, -1.0, A.mult, reads=["lf"], writes=["lo"])
+        if u > 0:
+            addl(u - 1)
+        second_part(u)
+    first_part(15)
+    level(14, 8)
+    product(15, 2, 0, 320)
+    for k in (1, 2, 3):
+        level(15, k)
+    addl(14)
+    product(15, 2, 320, 512)
+    level(15, 4)
+    for j in (1, 2, 3):
+        level(15, 4 + j)
+        need("g", deps("g", ["u%d0" % j, "u%d1" % j], (), ()))
+        sent[0] += send(g, T, topo, core, T.cores[(rank + j) % N], T["uin%d" % j][:], T["uout%d" % j][:], "ua")
+    level(15, 8)
+    product(15, 2, 512, 1024)
+    addl(15)
+    steps = energies(0, slice(0, 128), "0")
+    next(steps)
+    cp("vd", T.invi[:], T.invl[:], reads=["invl"], writes=["invi"])
+    next(steps)
+    ts("ve", T.inv16[:], T.invi[:], -512.0, A.add, reads=["invi"], writes=["inv16"])
+    next(steps)
+
+    uin = [T["uin%d" % j] for j in range(4)]
+    for h in range(2):
+        tok = None
+        for j in range(4):
+            tok = mms("n%d" % h, [(ps[6 + h][:, j:512:4], T.idn[:], uin[i][:, 128 * h:128 * h + 128], i == 0, i == j) for i in range(j + 1)],
+                      reads=["idn", "u00", "u01"] + (["uin"] if j else []), writes=["n%d" % h], bank=[6 + h], tok=tok)
+    for h in range(2):
+        c = slice(512 * h, 512 * h + 512)
+        op("v", "sm%d" % h, lambda: V.tensor_tensor_scan(T.scm[:, c], T.rst[:], ps[6 + h][:], 0.0, A.mult, A.min), reads=["rst", "n%d" % h], writes=["scm%d" % h], bank=[6 + h])
+        op("v", "sz%d" % h, lambda: V.tensor_tensor_scan(T.scz[:, c], T.rst[:], ps[6 + h][:], 0.0, A.mult, A.max), reads=["rst", "n%d" % h], writes=["scz%d" % h], bank=[6 + h])
+        ts("tc%d" % h, T.tt[:, 128 * h:128 * h + 128], ps[6 + h][:, 3:512:4], -1.0, A.mult, reads=["n%d" % h], writes=["tt%d" % h], bank=[6 + h])
+
+    def spread(r):
+        h = r % 2
+        w = T.wp[:, 128 * r:128 * r + 128]
+        tok = mms("uz%d" % h, [(ps[4 + h][:, 0:256], w, T.scm[:, 3:1024:4], True, True)], reads=["wp", "scm0", "scm1"], writes=["U%d" % h], bank=[4 + h])
+        mms("uz%d" % h, [(ps[4 + h][:, 256:512], w, T.scz[:, 3:1024:4], True, True)], reads=["wp", "scz0", "scz1"], writes=["U%d" % h], bank=[4 + h], tok=tok)
+
+    spread(0)
+    spread(1)
+    for r in range(16):
+        h = r % 2
+        H = str(h)
+        tt("g" + H, T["gb" + H][:], T.ac15[:, r:4096:16], ps[4 + h][:, 0:256], A.min, reads=["ac15", "U" + H], writes=["gb" + H], bank=[4 + h])
+        tt("mm" + H, T["mb" + H][:], T.acor[:, r:4096:16], ps[4 + h][:, 256:512], A.is_gt, reads=["acor", "U" + H], writes=["mb" + H], bank=[4 + h])
+        if r + 2 < 16:
+            spread(r + 2)
+        X = ps[6 + h][:, 0:256]
+        mms("xx" + H, [(X, T.wp[:, 128 * r:128 * r + 128], T.tt[:], True, False), (X, T.idb[:], T["gb" + H][:], False, False),
+                       (X, T.id32[:], T["mb" + H][:], False, True)],
+            reads=["wp", "tt0", "tt1", "idb", "id32", "gb" + H, "mb" + H], writes=["X" + H], bank=[6 + h])
+        op("s", "f" + H, lambda: S.activation(T.fn[:, 256 * r:256 * r + 256], X, AF.Relu, bias=-17.0), reads=["X" + H], writes=["fn%d" % r], bank=[6 + h])
+    fn = ["fn%d" % r for r in range(16)]
+    order = (0, 2, 1, 3, 4, 6, 5, 7)
+    for p in order:
+        out = T.slb0[:, 512 * p:512 * p + 512]
+        src = T.fn[:, 0:4096].indirect(T.inv16[:, 32 * p:32 * p + 32])
+        if p % 4 < 2:
+            cp("pm%d" % p, out, src, reads=fn + ["inv16"], writes=["slb0.%d" % p])
+        else:
+            op("s", "pm%d" % p, lambda: S.activation(out, src, AF.Copy), reads=fn + ["inv16"], writes=["slb0.%d" % p])
+    hand_out(1, order, lambda p: ["slb0.%d" % p])
+
+    def finish(h):
+        for i in range(2):
+            k = 2 * h + i
+            op("s", "ex%d" % i, lambda: S.activation(T.ylb[:, 512 * k:512 * k + 512], ps[k][:], AF.Exp, scale=-0.0078125),
+               reads=["L%d" % k], writes=["ylb%d" % k], bank=[k])
+            grp["st"] = op("y", "st", lambda: g.sync.dma_start(T.yl[:, 512 * k:512 * k + 512], T.ylb[:, 512 * k:512 * k + 512]),
+                           reads=["ylb%d" % k], inc=16, tok=grp.get("st"))
+
+    amounts(16)
+    amounts(17)
+    for u in range(16, 31):
+        first_part(u)
+        if u > 16:
+            addl(u - 1)
+        second_part(u)
+    addl(30)
+    finish(0)
+    product(31, 2, 0, 1024)
+    addl(31)
+    finish(1)
+    product(31, 1, 0, 1024)
+    loss(31)
+    level(31, 1)
+    for _ in energies(1, slice(128, 256), "1"):
+        pass
+    op("s", "st", lambda: S.dma_start(T.ye[:], T.yeb[:]), reads=["yeb0", "yeb1"], inc=16, tok=grp["st"])
+
+    g.wait_ge(T.sem.ls, sent[0])
+    for s, n in cnt.items():
+        if max(know[q].get(s, 0) for q in Q) < n:
+            g.wait_ge(T.sem[s], n)

@@ -23,6 +23,7 @@ for _n in ("idb", "id32", "idn", "c0", "cm", "sb"):
     SCRATCH[_n] = ("sbuf", [128, 128], BF)
 for _h in range(2):
     SCRATCH["am%d" % _h] = ("sbuf", [128, 1024], BF)
+    SCRATCH["kg%d" % _h] = ("sbuf", [128, 1024], BF)
     SCRATCH["pa%d" % _h] = ("sbuf", [128, 1024], BF)
     SCRATCH["pb%d" % _h] = ("sbuf", [128, 1024], F32)
     SCRATCH["gb%d" % _h] = ("sbuf", [128, 256], BF)
@@ -40,7 +41,7 @@ SCRATCH.update({
 })
 
 _HALF = ["pa", "pb", "c1", "c2", "en", "m", "e", "mx", "my", "e16", "x", "y", "vx", "vy", "v", "v16", "ka", "kb",
-         "aa", "ab", "d", "l", "uz", "g", "mm", "xx", "f", "n", "sm", "sz", "tc", "ex", "uu"]
+         "aa", "ab", "d", "l", "uz", "g", "mm", "xx", "f", "n", "sm", "sz", "tc", "ex", "kc", "kd", "ap"]
 SEMAPHORES = ([n + str(h) for n in _HALF for h in range(2)]
               + ["ld%d" % p for p in range(8)] + ["li%d" % p for p in range(7)] + ["pm%d" % p for p in range(8)]
               + ["va", "vb", "vc", "vd", "ve", "vf", "ga", "gb", "gc0", "gd", "ge", "gi0", "gi1", "gi2", "gi3",
@@ -310,12 +311,10 @@ def rank_program(g, core, T, topo):
     def side(u):
         if 1 <= u <= 14:
             scatter(u + 1)
-        if 1 <= u <= 8:
-            i = u - 1
+        for i in {1: (0,), 15: range(1, 8)}.get(u, ()):
             grp["aco"] = op("s", "aco", lambda: S.activation(T.acor[:, 512 * i:512 * i + 512], T.tab0[:, 0:4096].indirect(T.cor16[:, 32 * i:32 * i + 32]), AF.Copy),
                             reads=["cor16"] + own[0], writes=["acor"], tok=grp.get("aco"))
-        if 10 <= u <= 13:
-            i = u - 10
+        for i in range(4 if u == 15 else 0):
             grp["a15"] = op("s", "a15", lambda: S.activation(T.ac15[:, 1024 * i:1024 * i + 1024], T.acor[:, 1024 * i:1024 * i + 1024], AF.Identity, bias=-15.0),
                             reads=["acor"], writes=["ac15"], tok=grp.get("a15"))
         if u == 14:
@@ -348,9 +347,33 @@ def rank_program(g, core, T, topo):
         t = tables(u)
         name = ("pa", "pb")[which - 1] + str(h)
         key = (name, u)
+        if which == 2 and lo // 512 in lifted(u):
+            i = lo // 512
+            grp[key] = tt(name, T[name][:, lo:hi], T["kg%d" % h][:, lo:hi], ps[6 + i][:, lo - 512 * i:hi - 512 * i], A.mult,
+                          reads=["kg%d.%d" % (h, i), "ap%d" % i], writes=[name], bank=[6 + i], tok=grp.get(key))
+            return
         grp[key] = tt(name, T[name][:, lo:hi], t[which].indirect(T.e16[:, 64 * u + lo // 16:64 * u + hi // 16]), T["am%d" % h][:, lo:hi], A.mult,
                       reads=t[3][which] + ["e16.%d" % u] + ["am%d.%d" % (h, i) for i in range(lo // 512, (hi - 1) // 512 + 1)],
                       writes=[name], tok=grp.get(key))
+
+    def lifted(u):
+        if u in (0, 1, 15, 16, 17, 31):
+            return ()
+        return (1,) if u < 16 else (0, 1)
+
+    def coefficients(u):
+        h = u % 2
+        t = tables(u)
+        for i in lifted(u):
+            op("s", ("kc", "kd")[i] + str(h),
+               lambda: S.activation(T["kg%d" % h][:, 512 * i:512 * i + 512], t[2].indirect(T.e16[:, 64 * u + 32 * i:64 * u + 32 * i + 32]), AF.Copy),
+               reads=t[3][2] + ["e16.%d" % u], writes=["kg%d.%d" % (h, i)])
+
+    def lift(u):
+        h = u % 2
+        for i in lifted(u):
+            mms("ap%d" % i, [(ps[6 + i][:], T.idb[:], T["am%d" % h][:, 512 * i:512 * i + 512], True, True)],
+                reads=["idb", "am%d.%d" % (h, i)], writes=["ap%d" % i], bank=[6 + i])
 
     def loss(u):
         h = u % 2
@@ -406,11 +429,10 @@ def rank_program(g, core, T, topo):
             return
         if k == 2:
             tt("m" + H, m, T.c1[:, c], c2, A.add, reads=["c1" + H, "c2" + H], writes=["m" + H], bank=bk)
-            ts("e" + H, T.ee[:, c], T.le[:, cb], 6, A.arith_shift_right, reads=[kE], writes=["ee" + H])
+            ts("e16" + H, T.e16[:, 64 * (u + 2):64 * (u + 2) + 64], T.le[:, cb], 0.015625, A.mult, -0.4921875, A.add, reads=[kE], writes=["e16.%d" % (u + 2)])
         if k == 3:
             tt("mx" + H, mx, T.ldx[:, cb], m, A.mult, reads=["ldx", "m" + H], writes=["mx" + H], bank=bk)
             tt("my" + H, my, T.dy4[:, cb], m, A.mult, reads=["dy4", "m" + H], writes=["my" + H], bank=bk)
-            cp("e16" + H, T.e16[:, 64 * (u + 2):64 * (u + 2) + 64], T.ee[:, c], reads=["ee" + H], writes=["e16.%d" % (u + 2)])
             if u in (12, 13):
                 tt("c2" + H, T.ef[:, c], T.le[:, cb], T.lf[:, c], A.subtract, reads=[kE, "lf"], writes=["ef" + H])
         if k == 4:
@@ -435,20 +457,24 @@ def rank_program(g, core, T, topo):
 
     def first_part(u):
         prev = u - 1 if u % 16 else -1
-        for i in range(4):
-            product(u, 1, 256 * i, 256 * i + 256)
-            if i == 3:
+        cut = (0, 160, 320, 512, 672, 832, 1024)
+        for i in range(6):
+            product(u, 1, cut[i], cut[i + 1])
+            if i == 5:
+                lift(u)
                 loss(u)
-            level(prev, 4 + i)
+            level(prev, 2 + i)
+            if i == 0 and prev >= 0 and u % 16 < 15:
+                coefficients(u + 1)
         if prev >= 0:
             if u % 16 < 15:
                 amounts(u + 1)
             bands(prev)
 
     def second_part(u):
-        for k, (lo, hi) in enumerate(((0, 640), (640, 832), (832, 1024))):
-            product(u, 2, lo, hi)
-            level(u, 1 + k)
+        for i in range(2):
+            product(u, 2, 512 * i, 512 * i + 512)
+        level(u, 1)
 
     def energies(b, c, tag):
         keys = ["E%d%d" % (b, h) for h in range(2)]

@@ -11,45 +11,56 @@ for _j in range(N):
     SCRATCH["slb%d" % _j] = ("sbuf", [128, 4096], BF)
     SCRATCH["uin%d" % _j] = ("sbuf", [128, 256], BF)
     SCRATCH["uout%d" % _j] = ("sbuf", [128, 256], BF)
-for _n in ("lx", "ly", "ldx", "ldy", "le", "lcor", "y4", "dy4", "ta", "tb", "tc", "td", "invi"):
+    SCRATCH["pq%d" % _j] = ("sbuf", [128, 512], F32)
+for _n in ("lx", "ly", "ldx", "ldy", "le", "lcor", "y4", "dx2", "dy8", "ta", "tb", "tc", "td", "invi"):
     SCRATCH[_n] = ("sbuf", [128, 256], I32)
-for _n in ("lf", "ci", "ef", "lo", "c1", "ee", "vxb", "vyb", "vb", "df"):
+for _n in ("lf", "ci", "cb", "ef", "lo", "c1", "vxb", "vyb", "vb", "df"):
     SCRATCH[_n] = ("sbuf", [128, 128], I32)
 for _n in ("cor16", "coro16", "inv16"):
     SCRATCH[_n] = ("sbuf", [128, 256], U16)
 for _n in ("v16", "e16"):
     SCRATCH[_n] = ("sbuf", [128, 2048], U16)
-for _n in ("idb", "id32", "idn", "c0", "cm", "sb"):
+for _n in ("idb", "id32", "idn", "c0", "cm", "sb", "blk"):
     SCRATCH[_n] = ("sbuf", [128, 128], BF)
 for _h in range(2):
     SCRATCH["am%d" % _h] = ("sbuf", [128, 1024], BF)
     SCRATCH["kg%d" % _h] = ("sbuf", [128, 1024], BF)
     SCRATCH["pa%d" % _h] = ("sbuf", [128, 1024], BF)
-    SCRATCH["pb%d" % _h] = ("sbuf", [128, 1024], F32)
+    SCRATCH["pb%d" % _h] = ("sbuf", [128, 512], F32)
+    SCRATCH["lsb%d" % _h] = ("sbuf", [128, 512], F32)
+for _h in range(3):
     SCRATCH["gb%d" % _h] = ("sbuf", [128, 256], BF)
     SCRATCH["mb%d" % _h] = ("sbuf", [128, 256], BF)
 for _b in range(8):
     SCRATCH["ps%d" % _b] = ("psum", [128, 512], F32)
 SCRATCH.update({
     "ones": ("sbuf", [128, 128], F32), "idf": ("sbuf", [128, 128], F32),
-    "b8a": ("sbuf", [128, 8], F32), "b8b": ("sbuf", [128, 8], F32),
     "qq": ("sbuf", [128, 144], BF), "wp": ("sbuf", [128, 2048], BF), "rst": ("sbuf", [128, 512], F32),
     "iot": ("sbuf", [128, 4096], F32), "invr": ("sbuf", [128, 4096], F32), "invl": ("sbuf", [128, 256], F32),
-    "acor": ("sbuf", [128, 4096], BF), "ac15": ("sbuf", [128, 4096], BF), "fn": ("sbuf", [128, 4096], BF),
+    "acor": ("sbuf", [128, 4096], BF), "fn": ("sbuf", [128, 4096], BF),
     "mk": ("sbuf", [128, 1024], BF), "scm": ("sbuf", [128, 1024], BF), "scz": ("sbuf", [128, 1024], BF),
-    "tt": ("sbuf", [128, 256], BF), "ylb": ("sbuf", [128, 2048], F32), "yeb": ("sbuf", [128, 256], F32),
+    "tt": ("sbuf", [128, 256], BF), "uu": ("sbuf", [128, 256], BF),
+    "ylb": ("sbuf", [128, 2048], F32), "yeb": ("sbuf", [128, 256], F32),
 })
 
-_HALF = ["pa", "pb", "c1", "c2", "en", "m", "e", "mx", "my", "e16", "x", "y", "vx", "vy", "v", "v16", "ka", "kb",
-         "aa", "ab", "d", "l", "uz", "g", "mm", "xx", "f", "n", "sm", "sz", "tc", "ex", "kc", "kd", "ap"]
+_HALF = ["pa", "pb", "pc", "c1", "c2", "en", "m", "mx", "my", "e16", "x", "y", "vx", "vy", "v", "v16", "ka", "kb",
+         "aa", "ab", "ac", "d", "l", "uz", "g", "mm", "xx", "f", "n", "sm", "sz", "tc", "ex", "kc", "ap"]
 SEMAPHORES = ([n + str(h) for n in _HALF for h in range(2)]
-              + ["ld%d" % p for p in range(8)] + ["li%d" % p for p in range(7)] + ["pm%d" % p for p in range(8)]
-              + ["va", "vb", "vc", "vd", "ve", "vf", "ga", "gb", "gc0", "gd", "ge", "gi0", "gi1", "gi2", "gi3",
-                 "sct", "aco", "a15", "ivd", "st", "ls", "ua"]
-              + ["tb%d%d" % (b, j) for b in range(2) for j in (1, 2, 3)]
-              + ["ha%d" % i for i in range(4)] + ["rl%d" % i for i in range(8)])
+              + ["ld%d" % p for p in range(6)] + ["li%d" % p for p in range(6)] + ["pm%d" % p for p in range(8)]
+              + ["va", "vb", "vc", "vd", "ve", "vf", "vw", "gb", "gd", "ge", "gi0", "gi1", "gi2", "gi3",
+                 "uz2", "g2", "mm2", "xx2", "f2", "sct", "aco", "ivd", "st", "ls", "ua0", "ua1", "sa", "sk"]
+              + ["tb%d%d" % (b, j) for b in range(2) for j in (1, 2, 3)] + ["dl%d" % i for i in range(4)]
+              + ["ha%d" % i for i in range(3)] + ["rl%d" % i for i in range(8)])
 
 PIECE = (768, 512)
+EARLY = 640
+LATE = (256, 384)
+SECOND = (3, 4)
+SLOT = (("loss", 0, 384), ("old", 4), ("loss", 384, 704), ("old", 5), ("loss", 704, 1024), ("old", 6), ("dose", 864, 1024), ("old", 7),
+        ("dose", 0, 512), ("new", 1), ("dose", 512, 672), ("new", 2), ("dose", 672, 864), ("new", 3))
+FRESH = (4,)
+LIFT = (608, 896)
+LIFT_BANKS = ((6, 7), (1, 3))
 
 
 def ways(T, topo):
@@ -75,7 +86,7 @@ def ways(T, topo):
 
 def parts(b, q, j):
     w = PIECE[b]
-    if j == 1:
+    if j == 1 and (b == 1 or q < 2):
         return [(2 * q * w, (2 * q + 1) * w), ((2 * q + 1) * w, (2 * q + 2) * w)]
     return [(2 * q * w, (2 * q + 2) * w)]
 
@@ -117,8 +128,10 @@ def helper_program(g, core, T, topo):
             for b in range(2):
                 for j in (1, 2, 3):
                     for i in range(len(parts(b, q, j))):
-                        if j == 1:
-                            g.wait_ge(T.sem["ha%d" % (2 * b + i)], k)
+                        if j == 1 and b == 1:
+                            g.wait_ge(T.sem["ha%d" % (1 + i)], k)
+                        elif j == 1 and i == 0:
+                            g.wait_ge(T.sem.ha0, k if q == 2 else len(topo.engines(c, core)))
                         sent += send_part(g, T, topo, relay, r, core, b, q, j, i)
     for b in range(2):
         for j in (1, 2, 3):
@@ -220,21 +233,27 @@ def rank_program(g, core, T, topo):
     def load(q, sem, out, in_, key, tok=None):
         return op(q, sem, lambda: Q[q].dma_start(out, in_), writes=[key], inc=16, tok=tok)
 
-    load("s", "li0", T.lx[:], T.px[:], "lx")
-    load("s", "li1", T.ly[:], T.py[:], "ly")
-    load("s", "li2", T.le[:], T.en[:], "le")
     load("s", "li3", T.lcor[:], T.cor[:], "lcor")
+    lists = ((T.lx, T.px, "lx"), (T.ly, T.py, "ly"), (T.le, T.en, "le"), (T.ldx, T.vx, "ldx"), (T.ldy, T.vy, "ldy"))
+    for i, (buf, t, key) in enumerate(lists[:3]):
+        load("s", "li%d" % i, buf[:, 0:128], t[:, 0:128], key + "0")
     srcs = ((0, 4096, T.slab), (4096, 5120, T.spow), (5120, 6144, T.kap))
-    for p in range(8):
-        tok = None
-        for a, z, t in srcs:
-            lo, hi = max(a, 768 * p), min(z, 768 * p + 768)
+    for q in range(4):
+        for i, (a, z, t) in enumerate(srcs):
+            lo, hi = max(a, 1536 * q), min(z, 1536 * q + 1536)
             if lo < hi:
-                tok = load("y", "ld%d" % p, T.tab0[:, lo:hi], t[:, lo - a:hi - a], "tab0.%d.%d" % (p, a), tok)
-    load("y", "li4", T.ldx[:], T.vx[:], "ldx")
-    load("y", "li5", T.ldy[:], T.vy[:], "ldy")
-    load("y", "li6", T.lf[:], T.fm[:], "lf")
-    own = {0: ["tab0.%d.0" % p for p in range(6)], 1: ["tab0.5.4096", "tab0.6.4096"], 2: ["tab0.6.5120", "tab0.7.5120"]}
+                load("y", "ld%d" % (q + i), T.tab0[:, lo:hi], t[:, lo - a:hi - a], "tab0.%d.%d" % (q, a))
+    tok = None
+    for buf, t, key in lists[3:]:
+        tok = load("y", "li4", buf[:, 0:128], t[:, 0:128], key + "0", tok)
+
+    def load_late(after):
+        need("y", deps("y", [after], (), ()))
+        tok = load("y", "li5", T.lf[:], T.fm[:], "lf")
+        for buf, t, key in lists:
+            tok = load("y", "li5", buf[:, 128:256], t[:, 128:256], key + "1", tok)
+
+    own = {0: ["tab0.%d.0" % q for q in range(3)], 1: ["tab0.2.4096", "tab0.3.4096"], 2: ["tab0.3.5120"]}
     for j in (1, 2, 3):
         for b in range(2):
             n = 0
@@ -244,84 +263,120 @@ def rank_program(g, core, T, topo):
                 last = senders[r][q] if last is None else last
                 n += len(parts(b, q, j)) * len(topo.engines(last, core))
             arrival("tb%d%d" % (b, j), n, "in%d%d" % (b, j))
-    arrival("ua", sum(len(topo.engines(T.cores[(rank - j) % N], core)) for j in (1, 2, 3)), "uin")
+    for h in range(2):
+        arrival("ua%d" % h, sum(len(topo.engines(T.cores[(rank - j) % N], core)) for j in (1, 2, 3)), "uin%d" % h)
 
     op("v", "va", lambda: V.memset(T.ones[:], 1.0), writes=["ones"])
     op("v", "vb", lambda: V.memset(T.qq[:], 0.0), writes=["qq"])
     op("v", "vc", lambda: V.memset(T.rst[:], 1.0), writes=["rst"])
-    op("g", "gi0", lambda: g.iota(T.iot[:, 0:1024], [[1, 64], [256, 16]], 512, 0, allow_small_or_imprecise_dtypes=True), writes=["iot0"])
-    op("g", "ga", lambda: g.affine_select(T.b8a[:], T.ones[:, 0:8], [[-16, 8]], A.is_ge, 0.0, 0, 1), reads=["ones"], writes=["b8a"])
+    op("g", "gi0", lambda: g.iota(T.iot[:, 0:1024], [[2, 64], [1, 2], [256, 8]], 512, 0, allow_small_or_imprecise_dtypes=True), writes=["iot0"])
     op("g", "gb", lambda: g.affine_select(T.idf[:], T.ones[:], [[-1, 128]], A.is_equal, 0.0, 0, 1), reads=["ones"], writes=["idf"])
-    op("g", "gc0", lambda: g.affine_select(T.b8b[:], T.b8a[:], [[16, 8]], A.is_ge, 0.0, 15, -1), reads=["b8a"], writes=["b8b"])
     op("g", "gd", lambda: g.iota(T.ci[:], [[0, 8], [-1, 16]], 128, 1), writes=["ci"])
+    op("g", "ge", lambda: g.iota(T.cb[:], [[-16, 8], [0, 16]], 128, 1), writes=["cb"])
     op("v", "vd", lambda: V.memset(T.rst[:, 0:512:4], 0.0), writes=["rst"])
-    ts("va", T.ta[:], T.lx[:], 4, A.arith_shift_right, reads=["lx"], writes=["ta"])
-    ts("vb", T.y4[:], T.ly[:], 4.0, A.mult, reads=["ly"], writes=["y4"])
-    ts("vc", T.tc[:], T.le[:], 6, A.arith_shift_right, reads=["le"], writes=["tc"])
-    ts("vd", T.tb[:], T.y4[:], 0xFC0, A.bitwise_and, reads=["y4"], writes=["tb"])
-    for b in range(2):
-        cp("ve", T.e16[:, 1024 * b:1024 * b + 128], T.tc[:, 128 * b:128 * b + 128], reads=["tc"], writes=["e16.%d" % (16 * b), "e16.%d" % (16 * b + 1)])
-        if b == 0:
-            tt("va", T.td[:], T.ta[:], T.tb[:], A.add, reads=["ta", "tb"], writes=["td"])
-    for b in range(2):
-        cp("vf", T.v16[:, 1024 * b:1024 * b + 128], T.td[:, 128 * b:128 * b + 128], reads=["td"], writes=["v16.%d" % (16 * b), "v16.%d" % (16 * b + 1)])
-        if b == 0:
-            ts("vb", T.ta[:], T.lcor[:], 15, A.bitwise_and, reads=["lcor"], writes=["ta"])
+    ts("vb", T.ta[:], T.lcor[:], 15, A.bitwise_and, reads=["lcor"], writes=["ta"])
     ts("vc", T.tb[:], T.lcor[:], 4, A.arith_shift_right, reads=["lcor"], writes=["tb"])
     ts("vd", T.tc[:], T.ta[:], 256.0, A.mult, reads=["ta"], writes=["tc"])
-    cp("va", T.qq[:, 15:128:16], T.b8b[:], reads=["b8b"], writes=["qq"])
+
+    def by_halves(sem, out, in_, src, key):
+        tok = None
+        for k in range(4):
+            o = 128 * (k % 2) + 64 * (k // 2)
+            tok = cp(sem, out[:, o:o + 64], in_[:, 64 * k:64 * k + 64], reads=[src], writes=[key], tok=tok)
+
     tt("vb", T.td[:], T.tc[:], T.tb[:], A.add, reads=["tc", "tb"], writes=["td"])
-    cp("vc", T.cor16[:], T.lcor[:], reads=["lcor"], writes=["cor16"])
-    cp("vd", T.coro16[:], T.td[:], reads=["td"], writes=["coro16"])
+    by_halves("vc", T.cor16, T.lcor, "lcor", "cor16")
+    by_halves("vd", T.coro16, T.td, "td", "coro16")
+
+    def offsets(b):
+        B = str(b)
+        c = slice(128 * b, 128 * b + 128)
+        o = slice(1024 * b, 1024 * b + 128)
+        ts("va", T.ta[:, c], T.lx[:, c], 4, A.arith_shift_right, reads=["lx" + B], writes=["ta"])
+        ts("vb", T.y4[:, c], T.ly[:, c], 4.0, A.mult, reads=["ly" + B], writes=["y4" + B])
+        ts("vc", T.tc[:, c], T.le[:, c], 6, A.arith_shift_right, reads=["le" + B], writes=["tc"])
+        yield
+        ts("vd", T.tb[:, c], T.y4[:, c], 0xFC0, A.bitwise_and, reads=["y4" + B], writes=["tb"])
+        cp("ve", T.e16[:, o], T.tc[:, c], reads=["tc"], writes=["e16.%d" % (16 * b), "e16.%d" % (16 * b + 1)])
+        yield
+        tt("va", T.td[:, c], T.ta[:, c], T.tb[:, c], A.add, reads=["ta", "tb"], writes=["td"])
+        yield
+        cp("vf", T.v16[:, o], T.td[:, c], reads=["td"], writes=["v16.%d" % (16 * b), "v16.%d" % (16 * b + 1)])
+        yield
+
+    def strides(b):
+        B = str(b)
+        c = slice(128 * b, 128 * b + 128)
+        ts("va", T.dx2[:, c], T.ldx[:, c], 2.0, A.mult, reads=["ldx" + B], writes=["dx2" + B])
+        ts("vb", T.dy8[:, c], T.ldy[:, c], 8.0, A.mult, reads=["ldy" + B], writes=["dy8" + B])
+
+    steps = offsets(0)
+    next(steps)
     ts("ve", T.ci[:], T.ci[:], 15, A.bitwise_and, reads=["ci"], writes=["ci"])
+    ts("vw", T.cb[:], T.cb[:], 4, A.arith_shift_right, reads=["cb"], writes=["cb"])
+    next(steps)
+    ts("vw", T.blk[:], T.cb[:], 8.0, A.is_equal, reads=["cb"], writes=["blk"])
     ts("vf", T.cm[:], T.idf[:], 2.0, A.mult, reads=["idf"], writes=["cm"])
-    ts("va", T.c0[:], T.ci[:], 0.0, A.is_equal, reads=["ci"], writes=["c0"])
+    next(steps)
     cp("vb", T.idb[:], T.idf[:], reads=["idf"], writes=["idb"])
     ts("vc", T.id32[:], T.idf[:], 32.0, A.mult, reads=["idf"], writes=["id32"])
+    next(steps)
+    ts("va", T.c0[:], T.ci[:], 0.0, A.is_equal, reads=["ci"], writes=["c0"])
     ts("vd", T.idn[:], T.idf[:], -1.0, A.mult, reads=["idf"], writes=["idn"])
     tt("ve", T.cm[:], T.cm[:], T.c0[:], A.add, reads=["cm", "c0"], writes=["cm"])
+    cp("vf", T.qq[:, 15:128:16], T.blk[:, 0:128:16], reads=["blk"], writes=["qq"])
+    tok = None
+    for r in range(16):
+        tok = ts("vw", T.wp[:, 128 * r:128 * r + 128], T.blk[:], T.c0[:, r:r + 1], A.mult, reads=["blk", "c0"], writes=["wp"], tok=tok)
 
-    spare = spare_mask(topo, core, senders[rank][0], T.cores[(rank + 1) % N])
+    lanes = (spare_mask(topo, core, senders[rank][0], T.cores[(rank + 1) % N]), topo.mask(core, T.cores[(rank + 1) % N]))
 
-    def hand_out(b, order, keys):
-        name = ("tab0", "slb0")[b]
-        w = PIECE[b]
+    def hand_out_tables():
+        for q in range(4):
+            need("g", deps("g", ["tab0.%d.%d" % (q, a) for a in (0, 4096, 5120)], (), ()))
+            buf = T.tab0[:, 2 * q * PIECE[0]:(2 * q + 2) * PIECE[0]]
+            if q < 3:
+                sent[0] += send(g, T, topo, core, senders[rank][q], buf, buf, "ha0", lanes[0] if q == 2 else None)
+        for j in (1, 2, 3):
+            sent[0] += send_part(g, T, topo, relay, rank, core, 0, 3, j, 0)
+
+    def hand_out_slab(order):
         for p in order:
-            need("g", deps("g", keys(p), (), ()))
+            need("g", deps("g", ["slb0.%d" % p], (), ()))
             if p < 6:
-                buf = T[name][:, p * w:(p + 1) * w]
-                sent[0] += send(g, T, topo, core, senders[rank][p // 2], buf, buf, "ha%d" % (2 * b + p % 2), spare)
+                buf = T.slb0[:, p * PIECE[1]:(p + 1) * PIECE[1]]
+                sent[0] += send(g, T, topo, core, senders[rank][p // 2], buf, buf, "ha%d" % (1 + p % 2), lanes[p in (1, 3)])
             else:
-                sent[0] += send_part(g, T, topo, relay, rank, core, b, 3, 1, p - 6)
+                sent[0] += send_part(g, T, topo, relay, rank, core, 1, 3, 1, p - 6)
         for j in (2, 3):
-            sent[0] += send_part(g, T, topo, relay, rank, core, b, 3, j, 0)
+            sent[0] += send_part(g, T, topo, relay, rank, core, 1, 3, j, 0)
 
-    hand_out(0, range(8), lambda p: ["tab0.%d.%d" % (p, a) for a in (0, 4096, 5120)])
+    hand_out_tables()
     for i in (1, 2, 3):
-        op("g", "gi%d" % i, lambda: g.iota(T.iot[:, 1024 * i:1024 * i + 1024], [[1, 64], [256, 16]], 512 + 64 * i, 0, allow_small_or_imprecise_dtypes=True), writes=["iot%d" % i])
-    op("g", "ge", lambda: g.iota(T.wp[:], [[0, 2048]], 1, 0, allow_small_or_imprecise_dtypes=True), writes=["wp"])
-    op("g", "ga", lambda: g.affine_select(T.wp[:], T.wp[:], [[-1, 16], [-16, 8], [0, 16]], A.is_equal, 0.0, 0, 1), reads=["wp"], writes=["wp"])
-
-    def scatter(i):
-        op("s", "sct", lambda: S.activation(T.invr[:, 0:4096].indirect(T.coro16[:, 16 * i:16 * i + 16]), T.iot[:, 256 * i:256 * i + 256], AF.Silu),
-           reads=["coro16", "iot%d" % (i // 4)], writes=["invr"])
+        op("g", "gi%d" % i, lambda: g.iota(T.iot[:, 1024 * i:1024 * i + 1024], [[2, 64], [1, 2], [256, 8]], 512 + 2048 * (i // 2) + 128 * (i % 2), 0,
+                                           allow_small_or_imprecise_dtypes=True), writes=["iot%d" % i])
 
     grp = {}
 
+    def scatter(lo, hi):
+        op("s", "sct", lambda: S.activation(T.invr[:, 0:4096].indirect(T.coro16[:, lo // 16:hi // 16]), T.iot[:, lo:hi], AF.Silu),
+           reads=["coro16"] + ["iot%d" % k for k in range(lo // 1024, (hi - 1) // 1024 + 1)], writes=["invr"])
+
     def side(u):
-        if 1 <= u <= 14:
-            scatter(u + 1)
-        for i in {1: (0,), 15: range(1, 8)}.get(u, ()):
-            grp["aco"] = op("s", "aco", lambda: S.activation(T.acor[:, 512 * i:512 * i + 512], T.tab0[:, 0:4096].indirect(T.cor16[:, 32 * i:32 * i + 32]), AF.Copy),
-                            reads=["cor16"] + own[0], writes=["acor"], tok=grp.get("aco"))
-        for i in range(4 if u == 15 else 0):
-            grp["a15"] = op("s", "a15", lambda: S.activation(T.ac15[:, 1024 * i:1024 * i + 1024], T.acor[:, 1024 * i:1024 * i + 1024], AF.Identity, bias=-15.0),
-                            reads=["acor"], writes=["ac15"], tok=grp.get("a15"))
+        mid = (4096 - EARLY - sum(LATE)) // 32
+        if 1 <= u < 14:
+            scatter(EARLY + 32 * (mid * (u - 1) // 13), EARLY + 32 * (mid * u // 13))
+        for h in range(2 if u == 14 else 0):
+            op("s", "ac%d" % h, lambda: S.activation(T.acor[:, 2048 * h:2048 * h + 2048], T.tab0[:, 0:4096].indirect(T.cor16[:, 128 * h:128 * h + 128]), AF.Copy),
+               reads=["cor16"] + own[0], writes=["acor%d" % h])
         if u == 14:
-            tok = None
-            for k in range(8):
-                tok = op("y", "ivd", lambda: g.sync.dma_start(T.invl[16 * k:16 * k + 16, :], T.invr[16 * k:16 * k + 1, :]),
-                         reads=["invr"], writes=["invl"], inc=16, tok=tok)
+            scatter(4096 - sum(LATE), 4096 - LATE[1])
+
+    def inverse():
+        tok = None
+        for k in range(8):
+            tok = op("y", "ivd", lambda: g.sync.dma_start(T.invl[16 * k:16 * k + 16, :], T.invr[16 * k:16 * k + 1, :]),
+                     reads=["invr"], writes=["invl"], inc=16, tok=tok)
 
     def tables(u):
         b, j = u // 16, (u % 16) // 4
@@ -333,47 +388,82 @@ def rank_program(g, core, T, topo):
             keys = [["in%d%d" % (b, j)], ["in0%d" % j], ["in0%d" % j]]
         return slab, tab[:, 4096:5120], tab[:, 5120:6144], keys
 
+    chunks = [x[1:] for x in SLOT if x[0] == "loss"]
+
+    def am_keys(u, lo, hi):
+        return ["am%d.%d" % (u % 2, a) for a, z in chunks if a < hi and lo < z]
+
     def amounts(u):
         h = u % 2
         slab, _, _, keys = tables(u)
-        for i in range(2):
-            op("s", ("aa", "ab")[i] + str(h),
-               lambda: S.activation(T["am%d" % h][:, 512 * i:512 * i + 512], slab.indirect(T.v16[:, 64 * u + 32 * i:64 * u + 32 * i + 32]), AF.Copy),
-               reads=keys[0] + ["v16.%d" % u], writes=["am%d.%d" % (h, i)])
-        side(u)
+        for i, (lo, hi) in enumerate(chunks):
+            op("s", ("aa", "ab", "ac")[i] + str(h),
+               lambda: S.activation(T["am%d" % h][:, lo:hi], slab.indirect(T.v16[:, 64 * u + lo // 16:64 * u + hi // 16]), AF.Copy),
+               reads=keys[0] + ["v16.%d" % u], writes=am_keys(u, lo, hi))
 
-    def product(u, which, lo, hi):
+    def plain(u):
+        if u in (0, 16):
+            return 1024
+        if u == 31:
+            return 512
+        return 1024 - LIFT[u // 16]
+
+    def losses(u, lo, hi):
         h = u % 2
         t = tables(u)
-        name = ("pa", "pb")[which - 1] + str(h)
-        key = (name, u)
-        if which == 2 and lo // 512 in lifted(u):
-            i = lo // 512
-            grp[key] = tt(name, T[name][:, lo:hi], T["kg%d" % h][:, lo:hi], ps[6 + i][:, lo - 512 * i:hi - 512 * i], A.mult,
-                          reads=["kg%d.%d" % (h, i), "ap%d" % i], writes=[name], bank=[6 + i], tok=grp.get(key))
-            return
-        grp[key] = tt(name, T[name][:, lo:hi], t[which].indirect(T.e16[:, 64 * u + lo // 16:64 * u + hi // 16]), T["am%d" % h][:, lo:hi], A.mult,
-                      reads=t[3][which] + ["e16.%d" % u] + ["am%d.%d" % (h, i) for i in range(lo // 512, (hi - 1) // 512 + 1)],
-                      writes=[name], tok=grp.get(key))
+        key = ("pa", u)
+        w, lst = (0, "v16") if u == 16 else (1, "e16")
+        grp[key] = tt("pa%d" % h, T["pa%d" % h][:, lo:hi], t[w].indirect(T[lst][:, 64 * u + lo // 16:64 * u + hi // 16]), T["am%d" % h][:, lo:hi], A.mult,
+                      reads=t[3][w] + ["%s.%d" % (lst, u)] + am_keys(u, lo, hi), writes=["pa%d" % h], tok=grp.get(key))
 
-    def lifted(u):
-        if u in (0, 1, 15, 16, 17, 31):
-            return ()
-        return (1,) if u < 16 else (0, 1)
+    def target(u, i):
+        h = u % 2
+        if i == 1 and u >= 30:
+            return ps[LIFT_BANKS[h][1]], "ap%d" % LIFT_BANKS[h][1]
+        name = "pb%d" % h if i == 0 else "lsb%d" % h if u < 2 else "pq%d" % (u % 4)
+        return T[name], name
+
+    def doses(u, lo, hi):
+        h = u % 2
+        t = tables(u)
+        for cut in (512, plain(u)):
+            if lo < cut < hi:
+                doses(u, lo, cut)
+                doses(u, cut, hi)
+                return
+        i = lo // 512
+        buf, name = target(u, i)
+        out = buf[:, lo - 512 * i:hi - 512 * i]
+        bank = LIFT_BANKS[h][i]
+        sem = ("pb", "pc")[i] + str(h)
+        key = (sem, u)
+        if lo >= plain(u):
+            grp[key] = tt(sem, out, T["kg%d" % h][:, lo:hi], ps[bank][:, lo - 512 * i:hi - 512 * i], A.mult,
+                          reads=["kg%d" % h, "ap%d" % bank], writes=[name], bank=[bank], tok=grp.get(key))
+        elif u == 16:
+            grp[key] = tt(sem, out, t[0].indirect(T.v16[:, 64 * u + lo // 16:64 * u + hi // 16]), T.kg0[:, lo:hi], A.mult,
+                          reads=t[3][0] + ["v16.%d" % u, "kg0"], writes=[name], tok=grp.get(key))
+        else:
+            grp[key] = tt(sem, out, t[2].indirect(T.e16[:, 64 * u + lo // 16:64 * u + hi // 16]), T["am%d" % h][:, lo:hi], A.mult,
+                          reads=t[3][2] + ["e16.%d" % u] + am_keys(u, lo, hi), writes=[name], tok=grp.get(key))
 
     def coefficients(u):
         h = u % 2
         t = tables(u)
-        for i in lifted(u):
-            op("s", ("kc", "kd")[i] + str(h),
-               lambda: S.activation(T["kg%d" % h][:, 512 * i:512 * i + 512], t[2].indirect(T.e16[:, 64 * u + 32 * i:64 * u + 32 * i + 32]), AF.Copy),
-               reads=t[3][2] + ["e16.%d" % u], writes=["kg%d.%d" % (h, i)])
+        lo = plain(u)
+        if lo < 1024:
+            op("s", "kc%d" % h,
+               lambda: S.activation(T["kg%d" % h][:, lo:1024], t[2].indirect(T.e16[:, 64 * u + lo // 16:64 * u + 64]), AF.Copy),
+               reads=t[3][2] + ["e16.%d" % u], writes=["kg%d" % h])
 
     def lift(u):
         h = u % 2
-        for i in lifted(u):
-            mms("ap%d" % i, [(ps[6 + i][:], T.idb[:], T["am%d" % h][:, 512 * i:512 * i + 512], True, True)],
-                reads=["idb", "am%d.%d" % (h, i)], writes=["ap%d" % i], bank=[6 + i])
+        for i in range(2):
+            lo, hi = max(plain(u), 512 * i), 512 * i + 512
+            if lo < hi:
+                bank = LIFT_BANKS[h][i]
+                mms("ap%d" % i, [(ps[bank][:, lo - 512 * i:512], T.idb[:], T["am%d" % h][:, lo:hi], True, True)],
+                    reads=["idb"] + am_keys(u, lo, hi), writes=["ap%d" % bank], bank=[bank])
 
     def loss(u):
         h = u % 2
@@ -382,176 +472,229 @@ def rank_program(g, core, T, topo):
 
     def addl(u):
         h = u % 2
-        tok = None
-        for i in range(2):
-            tok = op("t", "l%d" % h, lambda: PE.matmul(ps[2 * h + i][:], T.idf[:], T["pb%d" % h][:, 512 * i:512 * i + 512], u < 2, u >= 30),
-                     reads=["idf", "pb%d" % h], writes=["L%d" % (2 * h + i)], bank=[2 * h + i], tok=tok)
+        op("t", "l%d" % h, lambda: PE.matmul(ps[2 * h][:], T.idf[:], T["pb%d" % h][:], u < 2, u >= 30),
+           reads=["idf", "pb%d" % h], writes=["L%d" % h], bank=[2 * h])
+
+    def addl_dma(u):
+        if u >= 2:
+            op("g", "dl%d" % (u % 4), lambda: g.dma_start(T["lsb%d" % (u % 2)][:], T["pq%d" % (u % 4)][:], accum_op=A.add),
+               reads=["pq%d" % (u % 4)], writes=["lsb%d" % (u % 2)], inc=16)
+
+    def energy(u):
+        h, b = u % 2, u // 16
+        cb = slice(128 * b + 64 * h, 128 * b + 64 * h + 64)
+        kE = "E%d%d" % (b, h)
+        tt("en%d" % h, T.le[:, cb], T.le[:, cb], ps[4 + h][:, 0:64], A.subtract, reads=["le%d" % b, kE, "d%d" % h], writes=[kE], bank=[4 + h])
 
     def level(u, k):
-        if u < 0:
-            return
         h, b = u % 2, u // 16
         H = str(h)
         c = slice(64 * h, 64 * h + 64)
         cb = slice(128 * b + 64 * h, 128 * b + 64 * h + 64)
         P = ps[4 + h]
         bk = [4 + h]
-        d, c2, m, mx, my = P[:, 0:64], P[:, 64:128], P[:, 128:192], P[:, 192:256], P[:, 256:320]
+        d, m, mx, my = P[:, 0:64], P[:, 128:192], P[:, 192:256], P[:, 256:320]
         kE, kx, ky = "E%d%d" % (b, h), "x%d%d" % (b, h), "y%d%d" % (b, h)
-        last = u % 16 >= 14
         if k == 1:
-            if u in (14, 15):
-                tt("c1" + H, T.df[:, c], T.ef[:, c], d, A.subtract, reads=["ef" + H, "d" + H], writes=["df" + H], bank=bk)
-            if not last:
-                ts("c1" + H, T.c1[:, c], d, 800.0, A.is_lt, 2.0, A.mult, reads=["d" + H], writes=["c1" + H], bank=bk)
-                ts("c2" + H, c2, d, 1000.0, A.is_lt, 1.0, A.add, reads=["d" + H], writes=["c2" + H], bank=bk)
-            tt("en" + H, T.le[:, cb], T.le[:, cb], d, A.subtract, reads=["le", kE, "d" + H], writes=[kE], bank=bk)
-            return
-        if u in (14, 15):
-            Z = ps[6 + h]
-            if k == 2:
-                ts("m" + H, T.df[:, c], T.df[:, c], -1.0, A.max, 1.0, A.min, reads=["df" + H], writes=["df" + H])
-            if k == 3:
-                tt("mx" + H, T.sb[:, c], T.df[:, c], T.lo[:, c], A.max, reads=["df" + H, "lo"], writes=["sb" + H])
-                mms("uz" + H, [(Z[:, 0:64], T.cm[:], T.sb[:, c], True, True)], reads=["cm", "sb" + H], writes=["z" + H], bank=[6 + h])
-            if k == 4:
-                ts("x" + H, Z[:, 64:128], Z[:, 0:64], -1.0, A.max, 1.0, A.min, reads=["z" + H], writes=["t" + H], bank=[6 + h])
-            if k >= 5:
-                for j in {5: (1,), 6: (2,), 7: (3,), 8: (0,)}[k]:
-                    out = T["uout%d" % j] if j else T.uin0
-                    tok = None
-                    for kk in range(2):
-                        o = 128 * kk + 64 * h
-                        tok = tt(("vx", "vy", "v", "v16")[j] + H, out[:, o:o + 64], T.mk[:, 256 * j + o:256 * j + o + 64], Z[:, 64:128], A.mult,
-                                 reads=["t" + H, "mk%d%d%d" % (j, h, kk)], writes=["u%d%d" % (j, h)], bank=[6 + h], tok=tok)
-            return
-        if last:
-            return
+            ts("c1" + H, T.c1[:, c], d, -0.005, A.mult, 5.4975, A.add, reads=["d" + H], writes=["c1" + H], bank=bk)
+            energy(u)
         if k == 2:
-            tt("m" + H, m, T.c1[:, c], c2, A.add, reads=["c1" + H, "c2" + H], writes=["m" + H], bank=bk)
+            ts("m" + H, m, T.c1[:, c], 0.5, A.max, 2.0, A.min, reads=["c1" + H], writes=["m" + H], bank=bk)
             ts("e16" + H, T.e16[:, 64 * (u + 2):64 * (u + 2) + 64], T.le[:, cb], 0.015625, A.mult, -0.4921875, A.add, reads=[kE], writes=["e16.%d" % (u + 2)])
         if k == 3:
-            tt("mx" + H, mx, T.ldx[:, cb], m, A.mult, reads=["ldx", "m" + H], writes=["mx" + H], bank=bk)
-            tt("my" + H, my, T.dy4[:, cb], m, A.mult, reads=["dy4", "m" + H], writes=["my" + H], bank=bk)
-            if u in (12, 13):
-                tt("c2" + H, T.ef[:, c], T.le[:, cb], T.lf[:, c], A.subtract, reads=[kE, "lf"], writes=["ef" + H])
+            tt("mx" + H, mx, T.dx2[:, cb], m, A.mult, reads=["dx2%d" % b, "m" + H], writes=["mx" + H], bank=bk)
+            tt("my" + H, my, T.dy8[:, cb], m, A.mult, reads=["dy8%d" % b, "m" + H], writes=["my" + H], bank=bk)
         if k == 4:
-            tt("x" + H, T.lx[:, cb], T.lx[:, cb], mx, A.add, reads=["lx", kx, "mx" + H], writes=[kx], bank=bk)
-            tt("y" + H, T.y4[:, cb], T.y4[:, cb], my, A.add, reads=["y4", ky, "my" + H], writes=[ky], bank=bk)
+            tt("x" + H, T.lx[:, cb], T.lx[:, cb], mx, A.add, reads=["lx%d" % b, "v16.%d" % u, kx, "mx" + H], writes=[kx], bank=bk)
+            tt("y" + H, T.y4[:, cb], T.y4[:, cb], my, A.add, reads=["y4%d" % b, "v16.%d" % u, ky, "my" + H], writes=[ky], bank=bk)
         if k == 5:
             ts("vx" + H, T.vxb[:, c], T.lx[:, cb], 1023, A.bitwise_and, 4, A.arith_shift_right, reads=[kx], writes=["vxb" + H])
             ts("vy" + H, T.vyb[:, c], T.y4[:, cb], 0xFC0, A.bitwise_and, reads=[ky], writes=["vyb" + H])
         if k == 6:
             tt("v" + H, T.vb[:, c], T.vxb[:, c], T.vyb[:, c], A.add, reads=["vxb" + H, "vyb" + H], writes=["vb" + H])
+            if u in (12, 13):
+                tt("c2" + H, T.ef[:, c], T.le[:, cb], T.lf[:, c], A.subtract, reads=[kE, "lf"], writes=["ef" + H])
         if k == 7:
             cp("v16" + H, T.v16[:, 64 * (u + 2):64 * (u + 2) + 64], T.vb[:, c], reads=["vb" + H], writes=["v16.%d" % (u + 2)])
+            if u < 14 and (u // 2) % 2 == 0:
+                for kk in range(2):
+                    o = 256 * (u // 4) + 128 * h + 64 * kk
+                    ts(("ka", "kb")[kk] + H, T.mk[:, o:o + 64], T.vb[:, c], 2048.0, (A.is_lt, A.is_ge)[kk],
+                       reads=["vb" + H], writes=["mk%d%d%d" % (u // 4, h, kk)])
 
-    def bands(u):
-        if u < 0 or u >= 14 or (u // 2) % 2:
-            return
-        h, j = u % 2, u // 4
-        for kk in range(2):
-            o = 256 * j + 128 * kk + 64 * h
-            ts(("ka", "kb")[kk] + str(h), T.mk[:, o:o + 64], T.vb[:, 64 * h:64 * h + 64], 2048.0, (A.is_lt, A.is_ge)[kk],
-               reads=["vb%d" % h], writes=["mk%d%d%d" % (j, h, kk)])
+    def verdict(h, k):
+        H = str(h)
+        c = slice(64 * h, 64 * h + 64)
+        P = ps[4 + h]
+        bk = [4 + h]
+        d, z, t = P[:, 0:64], P[:, 320:384], P[:, 384:448]
+        if k == 1:
+            tt("c1" + H, T.df[:, c], T.ef[:, c], d, A.subtract, reads=["ef" + H, "d" + H], writes=["df" + H], bank=bk)
+            energy(14 + h)
+        if k == 2:
+            ts("m" + H, T.df[:, c], T.df[:, c], -1.0, A.max, 1.0, A.min, reads=["df" + H], writes=["df" + H])
+        if k == 3:
+            tt("mx" + H, T.sb[:, c], T.df[:, c], T.lo[:, c], A.max, reads=["df" + H, "lo"], writes=["sb" + H])
+            mms("uz" + H, [(z, T.cm[:], T.sb[:, c], True, True)], reads=["cm", "sb" + H], writes=["z" + H], bank=bk)
+        if k == 4:
+            ts("x" + H, t, z, -1.0, A.max, 1.0, A.min, reads=["z" + H], writes=["t" + H], bank=bk)
+        if k >= 5:
+            j = k - 5
+            out = T["uout%d" % j] if j else T.uin0
+            tok = None
+            for kk in range(2):
+                o = 128 * h + 64 * kk
+                tok = tt(("vx", "vy", "v", "v16")[j] + H, out[:, o:o + 64], T.mk[:, 256 * j + o:256 * j + o + 64], t, A.mult,
+                         reads=["t" + H, "mk%d%d%d" % (j, h, kk)], writes=["u%d%d" % (j, h)], bank=bk, tok=tok)
+            if j:
+                need("g", deps("g", ["u%d%d" % (j, h)], (), ()))
+                o = slice(128 * h, 128 * h + 128)
+                sent[0] += send(g, T, topo, core, T.cores[(rank + j) % N], T["uin%d" % j][:, o], out[:, o], "ua" + H)
 
-    def first_part(u):
-        prev = u - 1 if u % 16 else -1
-        cut = (0, 160, 320, 512, 672, 832, 1024)
-        for i in range(6):
-            product(u, 1, cut[i], cut[i + 1])
-            if i == 5:
-                lift(u)
-                loss(u)
-            level(prev, 2 + i)
-            if i == 0 and prev >= 0 and u % 16 < 15:
-                coefficients(u + 1)
-        if prev >= 0:
-            if u % 16 < 15:
-                amounts(u + 1)
-            bands(prev)
+    def exit_energy(u, k):
+        c = slice(128 * (u // 16) + 64 * (u % 2), 128 * (u // 16) + 64 * (u % 2) + 64)
+        ch = slice(64 * (u % 2), 64 * (u % 2) + 64)
+        H = str(u % 2)
+        if k == 2:
+            ts("c2" + H, T.vxb[:, ch], T.le[:, c], 0.0, A.max, reads=["E%d%s" % (u // 16, H)], writes=["vxb" + H])
+        if k == 3:
+            ts("ka" + H, T.vyb[:, ch], T.vxb[:, ch], 1023, A.bitwise_and, reads=["vxb" + H], writes=["vyb" + H])
+        if k == 4:
+            cp("kb" + H, T.yeb[:, c], T.vyb[:, ch], reads=["vyb" + H], writes=["yeb%d" % u])
 
-    def second_part(u):
-        for i in range(2):
-            product(u, 2, 512 * i, 512 * i + 512)
-        level(u, 1)
+    def follow(u, k):
+        if u in (14, 15):
+            for kk in {5: (6, 7), 6: (8,), 7: (5,)}.get(k, (k,)):
+                verdict(u % 2, kk)
+        elif u < 30:
+            level(u, k)
+        elif k == 1:
+            energy(u)
+        if u % 16 >= 14:
+            exit_energy(u, k)
 
-    def energies(b, c, tag):
-        keys = ["E%d%d" % (b, h) for h in range(2)]
-        ts("va", T.ta[:, c], T.le[:, c], 0.0, A.max, reads=keys, writes=["ta"])
-        yield
-        ts("vb", T.tb[:, c], T.ta[:, c], 1023, A.bitwise_and, reads=["ta"], writes=["tb"])
-        yield
-        cp("vc", T.yeb[:, c], T.tb[:, c], reads=["tb"], writes=["yeb" + tag])
-        yield
+    def ahead(u, i):
+        t = tables(u)
+        w, c = 1 + i // 4, slice(256 * (i % 4), 256 * (i % 4) + 256)
+        name = ("am0", "kg0")[w - 1]
+        grp[name] = op("s", ("sa", "sk")[w - 1], lambda: S.activation(T[name][:, c], t[w].indirect(T.e16[:, 64 * u + 16 * (i % 4):64 * u + 16 * (i % 4) + 16]), AF.Copy),
+                       reads=t[3][w] + ["e16.%d" % u], writes=am_keys(u, 0, 1024) if w == 1 else ["kg0"], tok=grp.get(name))
 
-    scatter(0)
-    scatter(1)
-    amounts(0)
-    amounts(1)
-    for u in range(15):
-        first_part(u)
+    def start(u):
         if u == 0:
-            ts("va", T.dy4[:], T.ldy[:], 4.0, A.mult, reads=["ldy"], writes=["dy4"])
-        if u == 1:
-            ts("vb", T.lo[:], T.lf[:], 0.0, A.is_gt, -1.0, A.mult, reads=["lf"], writes=["lo"])
-        if u > 0:
-            addl(u - 1)
-        second_part(u)
-    first_part(15)
-    level(14, 8)
-    product(15, 2, 0, 320)
-    for k in (1, 2, 3):
-        level(15, k)
-    addl(14)
-    product(15, 2, 320, 512)
-    level(15, 4)
-    for j in (1, 2, 3):
-        level(15, 4 + j)
-        need("g", deps("g", ["u%d0" % j, "u%d1" % j], (), ()))
-        sent[0] += send(g, T, topo, core, T.cores[(rank + j) % N], T["uin%d" % j][:], T["uout%d" % j][:], "ua")
-    level(15, 8)
-    product(15, 2, 512, 1024)
-    addl(15)
-    steps = energies(0, slice(0, 128), "0")
+            amounts(u)
+        amounts(u + 1)
+        coefficients(u + 1)
+
+    def unit(u):
+        for x in SLOT:
+            if x[0] == "loss":
+                losses(u, x[1], x[2])
+                if x[2] == 1024:
+                    loss(u)
+                    if u % 16:
+                        addl(u - 1)
+            elif x[0] == "dose":
+                doses(u, x[1], x[2])
+            elif x[0] == "new":
+                follow(u, x[1])
+            elif u % 16:
+                follow(u - 1, x[1])
+                if x[1] == 7 and u % 16 < 15:
+                    amounts(u + 1)
+                    if u + 1 in FRESH:
+                        coefficients(u + 1)
+                if x[1] == 7 and u == 15:
+                    addl_dma(14)
+            elif u == 0 and x[1] == 7:
+                strides(0)
+        if u == 3:
+            load_late("v16.4")
+        if u == 8:
+            ts("vc", T.lo[:], T.lf[:], 0.0, A.is_gt, -1.0, A.mult, reads=["lf"], writes=["lo"])
+        if u % 16 < 15:
+            lift(u + 1)
+        if u % 16 < 14 and u + 2 not in FRESH:
+            coefficients(u + 2)
+        side(u)
+        if u < 30 and u not in (14, 15):
+            addl_dma(u)
+
+    scatter(0, EARLY)
+    start(0)
+    for u in range(16):
+        unit(u)
+    exit_energy(15, 4)
+    steps = offsets(1)
     next(steps)
-    cp("vd", T.invi[:], T.invl[:], reads=["invl"], writes=["invi"])
-    next(steps)
-    ts("ve", T.inv16[:], T.invi[:], -512.0, A.add, reads=["invi"], writes=["inv16"])
-    next(steps)
+    verdict(1, 4)
+    strides(1)
+    for k in (6, 7, 8, 5):
+        verdict(1, k)
+    for _ in steps:
+        pass
+    addl_dma(15)
+    grp["st"] = op("y", "st", lambda: g.sync.dma_start(T.ye[:, 0:128], T.yeb[:, 0:128]), reads=["yeb14", "yeb15"], inc=16)
 
     uin = [T["uin%d" % j] for j in range(4)]
-    for h in range(2):
+    ub, xb = (4, 5, 1), (3, 6)
+
+    def prefix(h):
         tok = None
         for j in range(4):
             tok = mms("n%d" % h, [(ps[6 + h][:, j:512:4], T.idn[:], uin[i][:, 128 * h:128 * h + 128], i == 0, i == j) for i in range(j + 1)],
-                      reads=["idn", "u00", "u01"] + (["uin"] if j else []), writes=["n%d" % h], bank=[6 + h], tok=tok)
-    for h in range(2):
+                      reads=["idn", "u0%d" % h] + (["uin%d" % h] if j else []), writes=["n%d" % h], bank=[6 + h], tok=tok)
+
+    def bounds(h):
         c = slice(512 * h, 512 * h + 512)
+        o = slice(128 * h, 128 * h + 128)
         op("v", "sm%d" % h, lambda: V.tensor_tensor_scan(T.scm[:, c], T.rst[:], ps[6 + h][:], 0.0, A.mult, A.min), reads=["rst", "n%d" % h], writes=["scm%d" % h], bank=[6 + h])
         op("v", "sz%d" % h, lambda: V.tensor_tensor_scan(T.scz[:, c], T.rst[:], ps[6 + h][:], 0.0, A.mult, A.max), reads=["rst", "n%d" % h], writes=["scz%d" % h], bank=[6 + h])
-        ts("tc%d" % h, T.tt[:, 128 * h:128 * h + 128], ps[6 + h][:, 3:512:4], -1.0, A.mult, reads=["n%d" % h], writes=["tt%d" % h], bank=[6 + h])
+        ts("vd", T.uu[:, o], T.scm[:, 512 * h + 3:512 * h + 512:4], 15.0, A.add, reads=["scm%d" % h], writes=["uu%d" % h])
+        ts("tc%d" % h, T.tt[:, o], ps[6 + h][:, 3:512:4], -1.0, A.mult, reads=["n%d" % h], writes=["tt%d" % h], bank=[6 + h])
 
-    def spread(r):
-        h = r % 2
-        w = T.wp[:, 128 * r:128 * r + 128]
-        tok = mms("uz%d" % h, [(ps[4 + h][:, 0:256], w, T.scm[:, 3:1024:4], True, True)], reads=["wp", "scm0", "scm1"], writes=["U%d" % h], bank=[4 + h])
-        mms("uz%d" % h, [(ps[4 + h][:, 256:512], w, T.scz[:, 3:1024:4], True, True)], reads=["wp", "scz0", "scz1"], writes=["U%d" % h], bank=[4 + h], tok=tok)
+    def row(i, par):
+        r = i % 8 + 8 * par
+        return T.wp[:, 128 * r:128 * r + 128]
 
-    spread(0)
-    spread(1)
-    for r in range(16):
-        h = r % 2
-        H = str(h)
-        tt("g" + H, T["gb" + H][:], T.ac15[:, r:4096:16], ps[4 + h][:, 0:256], A.min, reads=["ac15", "U" + H], writes=["gb" + H], bank=[4 + h])
-        tt("mm" + H, T["mb" + H][:], T.acor[:, r:4096:16], ps[4 + h][:, 256:512], A.is_gt, reads=["acor", "U" + H], writes=["mb" + H], bank=[4 + h])
-        if r + 2 < 16:
-            spread(r + 2)
-        X = ps[6 + h][:, 0:256]
-        mms("xx" + H, [(X, T.wp[:, 128 * r:128 * r + 128], T.tt[:], True, False), (X, T.idb[:], T["gb" + H][:], False, False),
-                       (X, T.id32[:], T["mb" + H][:], False, True)],
-            reads=["wp", "tt0", "tt1", "idb", "id32", "gb" + H, "mb" + H], writes=["X" + H], bank=[6 + h])
-        op("s", "f" + H, lambda: S.activation(T.fn[:, 256 * r:256 * r + 256], X, AF.Relu, bias=-17.0), reads=["X" + H], writes=["fn%d" % r], bank=[6 + h])
+    def spread(i):
+        h, k = i // 8, i % 3
+        tok = None
+        for o, src, key in ((256, T.scz[:, 512 * h + 3:512 * h + 512:4], "scz%d" % h), (0, T.uu[:, 128 * h:128 * h + 128], "uu%d" % h)):
+            for par in range(2):
+                tok = mms("uz%d" % k, [(ps[ub[k]][:, o + par:o + 256:2], row(i, par), src, True, True)], reads=["wp", key], writes=["U%d" % k], bank=[ub[k]], tok=tok)
+
+    prefix(0)
+    bounds(0)
+    for i in range(3):
+        spread(i)
+    for i in range(16):
+        h, k, x = i // 8, i % 3, i % 2
+        K = str(k)
+        a = T.acor[:, 2048 * h + i % 8:2048 * h + 2048:8]
+        tt("mm" + K, T["mb" + K][:], a, ps[ub[k]][:, 256:512], A.is_gt, reads=["acor%d" % h, "U" + K], writes=["mb" + K], bank=[ub[k]])
+        tt("g" + K, T["gb" + K][:], a, ps[ub[k]][:, 0:256], A.min, reads=["acor%d" % h, "U" + K], writes=["gb" + K], bank=[ub[k]])
+        if i == SECOND[1]:
+            bounds(1)
+        X = ps[xb[x]]
+        mms("xx%d" % x, [(X[:, 0:256], T.id32[:], T["mb" + K][:], True, False), (X[:, 0:256:2], row(i, 0), T.tt[:, 128 * h:128 * h + 128], False, False),
+                         (X[:, 1:256:2], row(i, 1), T.tt[:, 128 * h:128 * h + 128], False, False), (X[:, 0:256], T.idb[:], T["gb" + K][:], False, True)],
+            reads=["wp", "tt%d" % h, "idb", "id32", "gb" + K, "mb" + K], writes=["X%d" % x], bank=[xb[x]])
+        if i == SECOND[0]:
+            prefix(1)
+        if i + 3 < 16:
+            spread(i + 3)
+        op("s", "f%d" % x, lambda: S.activation(T.fn[:, 256 * i:256 * i + 256], X[:, 0:256], AF.Relu, bias=-32.0), reads=["X%d" % x], writes=["fn%d" % i], bank=[xb[x]])
+        if i < LATE[1] // 128:
+            scatter(4096 - LATE[1] + 128 * i, 4096 - LATE[1] + 128 * i + 128)
+        if i == LATE[1] // 128 - 1:
+            inverse()
+        if 5 <= i < 13:
+            ahead(16, i - 5)
+        if i == 14:
+            cp("vd", T.invi[:], T.invl[:], reads=["invl"], writes=["invi"])
+    ts("ve", T.inv16[:], T.invi[:], -512.0, A.add, reads=["invi"], writes=["inv16"])
+    addl(15)
     fn = ["fn%d" % r for r in range(16)]
     order = (0, 2, 1, 3, 4, 6, 5, 7)
     for p in order:
@@ -561,34 +704,38 @@ def rank_program(g, core, T, topo):
             cp("pm%d" % p, out, src, reads=fn + ["inv16"], writes=["slb0.%d" % p])
         else:
             op("s", "pm%d" % p, lambda: S.activation(out, src, AF.Copy), reads=fn + ["inv16"], writes=["slb0.%d" % p])
-    hand_out(1, order, lambda p: ["slb0.%d" % p])
+    hand_out_slab(order)
 
-    def finish(h):
-        for i in range(2):
-            k = 2 * h + i
-            op("s", "ex%d" % i, lambda: S.activation(T.ylb[:, 512 * k:512 * k + 512], ps[k][:], AF.Exp, scale=-0.0078125),
-               reads=["L%d" % k], writes=["ylb%d" % k], bank=[k])
-            grp["st"] = op("y", "st", lambda: g.sync.dma_start(T.yl[:, 512 * k:512 * k + 512], T.ylb[:, 512 * k:512 * k + 512]),
-                           reads=["ylb%d" % k], inc=16, tok=grp.get("st"))
+    def finish(h, i):
+        k = 2 * h + i
+        if i:
+            bank = LIFT_BANKS[h][1]
+            tt("mx%d" % h, T["lsb%d" % h][:], T["lsb%d" % h][:], ps[bank][:], A.add, reads=["lsb%d" % h, "ap%d" % bank], writes=["lsb%d" % h], bank=[bank])
+        src = T["lsb%d" % h] if i else ps[2 * h]
+        op("s", "ex%d" % i, lambda: S.activation(T.ylb[:, 512 * k:512 * k + 512], src[:], AF.Exp, scale=-0.0078125),
+           reads=["lsb%d" % h if i else "L%d" % h], writes=["ylb%d" % k], bank=[] if i else [2 * h])
+        grp["st"] = op("y", "st", lambda: g.sync.dma_start(T.yl[:, 512 * k:512 * k + 512], T.ylb[:, 512 * k:512 * k + 512]),
+                       reads=["ylb%d" % k], inc=16, tok=grp.get("st"))
 
-    amounts(16)
-    amounts(17)
+    start(16)
     for u in range(16, 31):
-        first_part(u)
-        if u > 16:
-            addl(u - 1)
-        second_part(u)
+        unit(u)
     addl(30)
-    finish(0)
-    product(31, 2, 0, 1024)
+    finish(0, 1)
+    follow(30, 4)
+    doses(31, 0, 512)
     addl(31)
-    finish(1)
-    product(31, 1, 0, 1024)
+    finish(0, 0)
+    finish(1, 0)
+    for lo, hi in chunks:
+        losses(31, lo, hi)
     loss(31)
-    level(31, 1)
-    for _ in energies(1, slice(128, 256), "1"):
-        pass
-    op("s", "st", lambda: S.dma_start(T.ye[:], T.yeb[:]), reads=["yeb0", "yeb1"], inc=16, tok=grp["st"])
+    doses(31, 512, 1024)
+    follow(31, 1)
+    finish(1, 1)
+    for k in (2, 3, 4):
+        follow(31, k)
+    op("y", "st", lambda: g.sync.dma_start(T.ye[:, 128:256], T.yeb[:, 128:256]), reads=["yeb30", "yeb31"], inc=16, tok=grp["st"])
 
     g.wait_ge(T.sem.ls, sent[0])
     for s, n in cnt.items():

from concourse.bass import DstId, RemoteDMATransfer
from concourse.mybir import dt, AluOpType, AxisListType, ActivationFunctionType

N = 4
SIM_CORES = 112
BF, F32, I32, U16 = "bfloat16", "float32", "int32", "uint16"

SCRATCH = {}
for _j in range(N):
    SCRATCH["tab%d" % _j] = ("sbuf", [128, 6144], BF)
    SCRATCH["slb%d" % _j] = ("sbuf", [128, 4096], BF)
    SCRATCH["uin%d" % _j] = ("sbuf", [128, 256], BF)
    SCRATCH["uout%d" % _j] = ("sbuf", [128, 256], BF)
    SCRATCH["pq%d" % _j] = ("sbuf", [128, 512], F32)
for _n in ("lx", "ly", "ldx", "ldy", "le", "lcor", "y4", "dx2", "dy8", "ta", "tb", "tc", "td", "invi"):
    SCRATCH[_n] = ("sbuf", [128, 256], I32)
for _n in ("lf", "ci", "cb", "ef", "lo", "c1", "vxb", "vyb", "vb", "df"):
    SCRATCH[_n] = ("sbuf", [128, 128], I32)
for _n in ("cor16", "coro16", "inv16"):
    SCRATCH[_n] = ("sbuf", [128, 256], U16)
for _n in ("v16", "e16"):
    SCRATCH[_n] = ("sbuf", [128, 2048], U16)
for _n in ("idb", "id32", "idn", "c0", "cm", "sb", "blk"):
    SCRATCH[_n] = ("sbuf", [128, 128], BF)
for _h in range(2):
    SCRATCH["am%d" % _h] = ("sbuf", [128, 1024], BF)
    SCRATCH["kg%d" % _h] = ("sbuf", [128, 1024], BF)
    SCRATCH["pa%d" % _h] = ("sbuf", [128, 1024], BF)
    SCRATCH["pb%d" % _h] = ("sbuf", [128, 512], F32)
    SCRATCH["lsb%d" % _h] = ("sbuf", [128, 512], F32)
for _h in range(3):
    SCRATCH["gb%d" % _h] = ("sbuf", [128, 256], BF)
    SCRATCH["mb%d" % _h] = ("sbuf", [128, 256], BF)
for _b in range(8):
    SCRATCH["ps%d" % _b] = ("psum", [128, 512], F32)
SCRATCH.update({
    "ones": ("sbuf", [128, 128], F32), "idf": ("sbuf", [128, 128], F32),
    "qq": ("sbuf", [128, 144], BF), "wp": ("sbuf", [128, 2048], BF), "rst": ("sbuf", [128, 512], F32),
    "iot": ("sbuf", [128, 4096], F32), "invr": ("sbuf", [128, 4096], F32), "invl": ("sbuf", [128, 256], F32),
    "acor": ("sbuf", [128, 4096], BF), "fn": ("sbuf", [128, 4096], BF),
    "mk": ("sbuf", [128, 1024], BF), "scm": ("sbuf", [128, 1024], BF), "scz": ("sbuf", [128, 1024], BF),
    "tt": ("sbuf", [128, 256], BF), "uu": ("sbuf", [128, 256], BF),
    "ylb": ("sbuf", [128, 2048], F32), "yeb": ("sbuf", [128, 256], F32),
})

_HALF = ["pa", "pb", "pc", "c1", "c2", "en", "m", "mx", "my", "e16", "x", "y", "vx", "vy", "v", "v16", "ka", "kb",
         "aa", "ab", "ac", "d", "l", "uz", "g", "mm", "xx", "f", "n", "sm", "sz", "tc", "ex", "kc", "ap"]
SEMAPHORES = ([n + str(h) for n in _HALF for h in range(2)]
              + ["ld%d" % p for p in range(6)] + ["li%d" % p for p in range(6)] + ["pm%d" % p for p in range(8)]
              + ["va", "vb", "vc", "vd", "ve", "vf", "vw", "gb", "gd", "ge", "gi0", "gi1", "gi2", "gi3",
                 "uz2", "g2", "mm2", "xx2", "f2", "sct", "aco", "ivd", "st", "ls", "ua0", "ua1", "sa", "sk"]
              + ["tb%d%d" % (b, j) for b in range(2) for j in (1, 2, 3)] + ["dl%d" % i for i in range(4)]
              + ["ha%d" % i for i in range(3)] + ["rl%d" % i for i in range(8)])

PIECE = (768, 512)
EARLY = 640
LATE = (256, 384)
SECOND = (3, 4)
SLOT = (("loss", 0, 384), ("old", 4), ("loss", 384, 704), ("old", 5), ("loss", 704, 1024), ("old", 6), ("dose", 864, 1024), ("old", 7),
        ("dose", 0, 512), ("new", 1), ("dose", 512, 672), ("new", 2), ("dose", 672, 864), ("new", 3))
FRESH = (4,)
LIFT = (608, 896)
LIFT_BANKS = ((6, 7), (1, 3))


def ways(T, topo):
    cores = T.cores
    senders = []
    for r in range(N):
        c = cores[r]
        able = [k for k in topo.cores_of(c) if k != c and all(topo.may_write(k, d) for d in cores if d != c)]
        near = [k for k in able if topo.die(k) == topo.die(c)]
        far = [k for k in able if topo.die(k) != topo.die(c)]
        senders.append([far[1], near[0], far[0], c])

    def relay(r, q, j):
        if q >= 2:
            return None
        d = cores[(r - j) % N]
        s = senders[r][q]
        able = [k for k in range(SIM_CORES) if topo.mates(topo.chip(k), topo.chip(d)) and topo.die(k) == topo.die(s)
                and topo.may_write(k, d) and topo.may_write(s, k)]
        return able[(j - 1) % len(able)]
    return senders, relay


def parts(b, q, j):
    w = PIECE[b]
    if j == 1 and (b == 1 or q < 2):
        return [(2 * q * w, (2 * q + 1) * w), ((2 * q + 1) * w, (2 * q + 2) * w)]
    return [(2 * q * w, (2 * q + 2) * w)]


def relay_sem(b, j, i):
    return "rl%d" % (4 * b + (i if j == 1 else j))


def send(g, T, topo, src, dst, out, in_, sem, mask=None):
    rid, pid = topo.addr(dst)[:2]
    m = topo.mask(src, dst) if mask is None else mask
    g.remote_dma(out, in_, T.sem[sem], T.sem.ls, pid, rid, m)
    return bin(m).count("1")


def send_part(g, T, topo, relay, r, src, b, q, j, i):
    name = ("tab%d", "slb%d")[b]
    lo, hi = parts(b, q, j)[i]
    via = relay(r, q, j)
    if via is None:
        return send(g, T, topo, src, T.cores[(r - j) % N], T[name % j][:, lo:hi], T[name % 0][:, lo:hi], "tb%d%d" % (b, j))
    return send(g, T, topo, src, via, T[name % j][:, lo:hi], T[name % 0][:, lo:hi], relay_sem(b, j, i))


def spare_mask(topo, src, near, far):
    off = topo.engines(src, far)
    return sum(1 << e for e in topo.engines(src, near) if e not in off)


def helper_program(g, core, T, topo):
    senders, relay = ways(T, topo)
    sent = 0
    for r in range(N):
        for q in range(3):
            if senders[r][q] != core:
                continue
            c = T.cores[r]
            k = bin(spare_mask(topo, c, core, T.cores[(r + 1) % N])).count("1")
            for b in range(2):
                for j in (1, 2, 3):
                    for i in range(len(parts(b, q, j))):
                        if j == 1 and b == 1:
                            g.wait_ge(T.sem["ha%d" % (1 + i)], k)
                        elif j == 1 and i == 0:
                            g.wait_ge(T.sem.ha0, k if q == 2 else len(topo.engines(c, core)))
                        sent += send_part(g, T, topo, relay, r, core, b, q, j, i)
    for b in range(2):
        for j in (1, 2, 3):
            for r in range(N):
                for q in range(2):
                    if relay(r, q, j) != core:
                        continue
                    d = T.cores[(r - j) % N]
                    for i, (lo, hi) in enumerate(parts(b, q, j)):
                        g.wait_ge(T.sem[relay_sem(b, j, i)], len(topo.engines(senders[r][q], core)))
                        buf = T[("tab%d", "slb%d")[b] % j][:, lo:hi]
                        sent += send(g, T, topo, core, d, buf, buf, "tb%d%d" % (b, j))
    if sent:
        g.wait_ge(T.sem.ls, sent)


def rank_program(g, core, T, topo):
    rank = T.rank_of(core)
    if rank is None:
        helper_program(g, core, T, topo)
        return
    A = AluOpType
    AF = ActivationFunctionType
    V, S, PE = g.vector, g.scalar, g.tensor
    Q = {"g": g, "v": V, "s": S, "t": PE, "y": g.sync}
    senders, relay = ways(T, topo)
    ps = [T["ps%d" % b] for b in range(8)]

    know = {q: {} for q in Q}
    cnt, lastw, readers, lastsem, banks = {}, {}, {}, {}, {}
    tick = [0]
    sent = [0]

    def need(q, toks):
        for t in sorted(toks, key=lambda t: -t["i"]):
            if know[q].get(t["s"], 0) < t["n"]:
                Q[q].wait_ge(T.sem[t["s"]], t["n"])
                for s, n in t["k"].items():
                    if know[q].get(s, 0) < n:
                        know[q][s] = n

    def deps(q, reads, writes, bank):
        d = [lastw[k] for k in list(reads) + list(writes) if k in lastw]
        for k in writes:
            d += readers.get(k, [])
        for b in bank:
            for e, ts in banks.get(b, {}).items():
                if e != q:
                    d += ts
        return d

    def op(q, sem, call, reads=(), writes=(), bank=(), inc=1, tok=None):
        d = deps(q, reads, writes, bank)
        if tok is None and sem in lastsem:
            d.append(lastsem[sem])
        need(q, [t for t in d if t is not tok])
        call().then_inc(T.sem[sem], inc)
        cnt[sem] = cnt.get(sem, 0) + inc
        tick[0] += 1
        if tok is None:
            tok = {"s": sem}
        tok["n"] = cnt[sem]
        tok["i"] = tick[0]
        tok["k"] = dict(know[q])
        tok["k"][sem] = cnt[sem]
        lastsem[sem] = tok
        for k in writes:
            lastw[k] = tok
            readers[k] = []
        for k in reads:
            readers.setdefault(k, []).append(tok)
        for b in bank:
            banks[b] = {q: banks.get(b, {}).get(q, []) + [tok]}
        return tok

    def arrival(sem, n, key):
        tick[0] += 1
        cnt[sem] = n
        lastw[key] = {"s": sem, "n": n, "i": tick[0], "k": {sem: n}}

    def ts(sem, out, in0, s1, op0, s2=None, op1=None, **kw):
        if op1 is None:
            return op("v", sem, lambda: V.tensor_scalar(out, in0, s1, None, op0), **kw)
        return op("v", sem, lambda: V.tensor_scalar(out, in0, s1, s2, op0, op1), **kw)

    def tt(sem, out, in0, in1, o, **kw):
        return op("v", sem, lambda: V.tensor_tensor(out, in0, in1, o), **kw)

    def cp(sem, out, in_, **kw):
        return op("v", sem, lambda: V.tensor_copy(out, in_), **kw)

    def mms(sem, group, **kw):
        def call():
            for a in group[:-1]:
                PE.matmul(*a)
            return PE.matmul(*group[-1])
        return op("t", sem, call, **kw)

    def load(q, sem, out, in_, key, tok=None):
        return op(q, sem, lambda: Q[q].dma_start(out, in_), writes=[key], inc=16, tok=tok)

    load("s", "li3", T.lcor[:], T.cor[:], "lcor")
    lists = ((T.lx, T.px, "lx"), (T.ly, T.py, "ly"), (T.le, T.en, "le"), (T.ldx, T.vx, "ldx"), (T.ldy, T.vy, "ldy"))
    for i, (buf, t, key) in enumerate(lists[:3]):
        load("s", "li%d" % i, buf[:, 0:128], t[:, 0:128], key + "0")
    srcs = ((0, 4096, T.slab), (4096, 5120, T.spow), (5120, 6144, T.kap))
    for q in range(4):
        for i, (a, z, t) in enumerate(srcs):
            lo, hi = max(a, 1536 * q), min(z, 1536 * q + 1536)
            if lo < hi:
                load("y", "ld%d" % (q + i), T.tab0[:, lo:hi], t[:, lo - a:hi - a], "tab0.%d.%d" % (q, a))
    tok = None
    for buf, t, key in lists[3:]:
        tok = load("y", "li4", buf[:, 0:128], t[:, 0:128], key + "0", tok)

    def load_late(after):
        need("y", deps("y", [after], (), ()))
        tok = load("y", "li5", T.lf[:], T.fm[:], "lf")
        for buf, t, key in lists:
            tok = load("y", "li5", buf[:, 128:256], t[:, 128:256], key + "1", tok)

    own = {0: ["tab0.%d.0" % q for q in range(3)], 1: ["tab0.2.4096", "tab0.3.4096"], 2: ["tab0.3.5120"]}
    for j in (1, 2, 3):
        for b in range(2):
            n = 0
            for q in range(4):
                r = (rank + j) % N
                last = relay(r, q, j)
                last = senders[r][q] if last is None else last
                n += len(parts(b, q, j)) * len(topo.engines(last, core))
            arrival("tb%d%d" % (b, j), n, "in%d%d" % (b, j))
    for h in range(2):
        arrival("ua%d" % h, sum(len(topo.engines(T.cores[(rank - j) % N], core)) for j in (1, 2, 3)), "uin%d" % h)

    op("v", "va", lambda: V.memset(T.ones[:], 1.0), writes=["ones"])
    op("v", "vb", lambda: V.memset(T.qq[:], 0.0), writes=["qq"])
    op("v", "vc", lambda: V.memset(T.rst[:], 1.0), writes=["rst"])
    op("g", "gi0", lambda: g.iota(T.iot[:, 0:1024], [[2, 64], [1, 2], [256, 8]], 512, 0, allow_small_or_imprecise_dtypes=True), writes=["iot0"])
    op("g", "gb", lambda: g.affine_select(T.idf[:], T.ones[:], [[-1, 128]], A.is_equal, 0.0, 0, 1), reads=["ones"], writes=["idf"])
    op("g", "gd", lambda: g.iota(T.ci[:], [[0, 8], [-1, 16]], 128, 1), writes=["ci"])
    op("g", "ge", lambda: g.iota(T.cb[:], [[-16, 8], [0, 16]], 128, 1), writes=["cb"])
    op("v", "vd", lambda: V.memset(T.rst[:, 0:512:4], 0.0), writes=["rst"])
    ts("vb", T.ta[:], T.lcor[:], 15, A.bitwise_and, reads=["lcor"], writes=["ta"])
    ts("vc", T.tb[:], T.lcor[:], 4, A.arith_shift_right, reads=["lcor"], writes=["tb"])
    ts("vd", T.tc[:], T.ta[:], 256.0, A.mult, reads=["ta"], writes=["tc"])

    def by_halves(sem, out, in_, src, key):
        tok = None
        for k in range(4):
            o = 128 * (k % 2) + 64 * (k // 2)
            tok = cp(sem, out[:, o:o + 64], in_[:, 64 * k:64 * k + 64], reads=[src], writes=[key], tok=tok)

    tt("vb", T.td[:], T.tc[:], T.tb[:], A.add, reads=["tc", "tb"], writes=["td"])
    by_halves("vc", T.cor16, T.lcor, "lcor", "cor16")
    by_halves("vd", T.coro16, T.td, "td", "coro16")

    def offsets(b):
        B = str(b)
        c = slice(128 * b, 128 * b + 128)
        o = slice(1024 * b, 1024 * b + 128)
        ts("va", T.ta[:, c], T.lx[:, c], 4, A.arith_shift_right, reads=["lx" + B], writes=["ta"])
        ts("vb", T.y4[:, c], T.ly[:, c], 4.0, A.mult, reads=["ly" + B], writes=["y4" + B])
        ts("vc", T.tc[:, c], T.le[:, c], 6, A.arith_shift_right, reads=["le" + B], writes=["tc"])
        yield
        ts("vd", T.tb[:, c], T.y4[:, c], 0xFC0, A.bitwise_and, reads=["y4" + B], writes=["tb"])
        cp("ve", T.e16[:, o], T.tc[:, c], reads=["tc"], writes=["e16.%d" % (16 * b), "e16.%d" % (16 * b + 1)])
        yield
        tt("va", T.td[:, c], T.ta[:, c], T.tb[:, c], A.add, reads=["ta", "tb"], writes=["td"])
        yield
        cp("vf", T.v16[:, o], T.td[:, c], reads=["td"], writes=["v16.%d" % (16 * b), "v16.%d" % (16 * b + 1)])
        yield

    def strides(b):
        B = str(b)
        c = slice(128 * b, 128 * b + 128)
        ts("va", T.dx2[:, c], T.ldx[:, c], 2.0, A.mult, reads=["ldx" + B], writes=["dx2" + B])
        ts("vb", T.dy8[:, c], T.ldy[:, c], 8.0, A.mult, reads=["ldy" + B], writes=["dy8" + B])

    steps = offsets(0)
    next(steps)
    ts("ve", T.ci[:], T.ci[:], 15, A.bitwise_and, reads=["ci"], writes=["ci"])
    ts("vw", T.cb[:], T.cb[:], 4, A.arith_shift_right, reads=["cb"], writes=["cb"])
    next(steps)
    ts("vw", T.blk[:], T.cb[:], 8.0, A.is_equal, reads=["cb"], writes=["blk"])
    ts("vf", T.cm[:], T.idf[:], 2.0, A.mult, reads=["idf"], writes=["cm"])
    next(steps)
    cp("vb", T.idb[:], T.idf[:], reads=["idf"], writes=["idb"])
    ts("vc", T.id32[:], T.idf[:], 32.0, A.mult, reads=["idf"], writes=["id32"])
    next(steps)
    ts("va", T.c0[:], T.ci[:], 0.0, A.is_equal, reads=["ci"], writes=["c0"])
    ts("vd", T.idn[:], T.idf[:], -1.0, A.mult, reads=["idf"], writes=["idn"])
    tt("ve", T.cm[:], T.cm[:], T.c0[:], A.add, reads=["cm", "c0"], writes=["cm"])
    cp("vf", T.qq[:, 15:128:16], T.blk[:, 0:128:16], reads=["blk"], writes=["qq"])
    tok = None
    for r in range(16):
        tok = ts("vw", T.wp[:, 128 * r:128 * r + 128], T.blk[:], T.c0[:, r:r + 1], A.mult, reads=["blk", "c0"], writes=["wp"], tok=tok)

    lanes = (spare_mask(topo, core, senders[rank][0], T.cores[(rank + 1) % N]), topo.mask(core, T.cores[(rank + 1) % N]))

    def hand_out_tables():
        for q in range(4):
            need("g", deps("g", ["tab0.%d.%d" % (q, a) for a in (0, 4096, 5120)], (), ()))
            buf = T.tab0[:, 2 * q * PIECE[0]:(2 * q + 2) * PIECE[0]]
            if q < 3:
                sent[0] += send(g, T, topo, core, senders[rank][q], buf, buf, "ha0", lanes[0] if q == 2 else None)
        for j in (1, 2, 3):
            sent[0] += send_part(g, T, topo, relay, rank, core, 0, 3, j, 0)

    def hand_out_slab(order):
        for p in order:
            need("g", deps("g", ["slb0.%d" % p], (), ()))
            if p < 6:
                buf = T.slb0[:, p * PIECE[1]:(p + 1) * PIECE[1]]
                sent[0] += send(g, T, topo, core, senders[rank][p // 2], buf, buf, "ha%d" % (1 + p % 2), lanes[p in (1, 3)])
            else:
                sent[0] += send_part(g, T, topo, relay, rank, core, 1, 3, 1, p - 6)
        for j in (2, 3):
            sent[0] += send_part(g, T, topo, relay, rank, core, 1, 3, j, 0)

    hand_out_tables()
    for i in (1, 2, 3):
        op("g", "gi%d" % i, lambda: g.iota(T.iot[:, 1024 * i:1024 * i + 1024], [[2, 64], [1, 2], [256, 8]], 512 + 2048 * (i // 2) + 128 * (i % 2), 0,
                                           allow_small_or_imprecise_dtypes=True), writes=["iot%d" % i])

    grp = {}

    def scatter(lo, hi):
        op("s", "sct", lambda: S.activation(T.invr[:, 0:4096].indirect(T.coro16[:, lo // 16:hi // 16]), T.iot[:, lo:hi], AF.Silu),
           reads=["coro16"] + ["iot%d" % k for k in range(lo // 1024, (hi - 1) // 1024 + 1)], writes=["invr"])

    def side(u):
        mid = (4096 - EARLY - sum(LATE)) // 32
        if 1 <= u < 14:
            scatter(EARLY + 32 * (mid * (u - 1) // 13), EARLY + 32 * (mid * u // 13))
        for h in range(2 if u == 14 else 0):
            op("s", "ac%d" % h, lambda: S.activation(T.acor[:, 2048 * h:2048 * h + 2048], T.tab0[:, 0:4096].indirect(T.cor16[:, 128 * h:128 * h + 128]), AF.Copy),
               reads=["cor16"] + own[0], writes=["acor%d" % h])
        if u == 14:
            scatter(4096 - sum(LATE), 4096 - LATE[1])

    def inverse():
        tok = None
        for k in range(8):
            tok = op("y", "ivd", lambda: g.sync.dma_start(T.invl[16 * k:16 * k + 16, :], T.invr[16 * k:16 * k + 1, :]),
                     reads=["invr"], writes=["invl"], inc=16, tok=tok)

    def tables(u):
        b, j = u // 16, (u % 16) // 4
        tab = T["tab%d" % j]
        slab = tab[:, 0:4096] if b == 0 else T["slb%d" % j][:, 0:4096]
        if j == 0:
            keys = [own[0] if b == 0 else ["slb0.%d" % p for p in range(8)], own[1], own[2]]
        else:
            keys = [["in%d%d" % (b, j)], ["in0%d" % j], ["in0%d" % j]]
        return slab, tab[:, 4096:5120], tab[:, 5120:6144], keys

    chunks = [x[1:] for x in SLOT if x[0] == "loss"]

    def am_keys(u, lo, hi):
        return ["am%d.%d" % (u % 2, a) for a, z in chunks if a < hi and lo < z]

    def amounts(u):
        h = u % 2
        slab, _, _, keys = tables(u)
        for i, (lo, hi) in enumerate(chunks):
            op("s", ("aa", "ab", "ac")[i] + str(h),
               lambda: S.activation(T["am%d" % h][:, lo:hi], slab.indirect(T.v16[:, 64 * u + lo // 16:64 * u + hi // 16]), AF.Copy),
               reads=keys[0] + ["v16.%d" % u], writes=am_keys(u, lo, hi))

    def plain(u):
        if u in (0, 16):
            return 1024
        if u == 31:
            return 512
        return 1024 - LIFT[u // 16]

    def losses(u, lo, hi):
        h = u % 2
        t = tables(u)
        key = ("pa", u)
        w, lst = (0, "v16") if u == 16 else (1, "e16")
        grp[key] = tt("pa%d" % h, T["pa%d" % h][:, lo:hi], t[w].indirect(T[lst][:, 64 * u + lo // 16:64 * u + hi // 16]), T["am%d" % h][:, lo:hi], A.mult,
                      reads=t[3][w] + ["%s.%d" % (lst, u)] + am_keys(u, lo, hi), writes=["pa%d" % h], tok=grp.get(key))

    def target(u, i):
        h = u % 2
        if i == 1 and u >= 30:
            return ps[LIFT_BANKS[h][1]], "ap%d" % LIFT_BANKS[h][1]
        name = "pb%d" % h if i == 0 else "lsb%d" % h if u < 2 else "pq%d" % (u % 4)
        return T[name], name

    def doses(u, lo, hi):
        h = u % 2
        t = tables(u)
        for cut in (512, plain(u)):
            if lo < cut < hi:
                doses(u, lo, cut)
                doses(u, cut, hi)
                return
        i = lo // 512
        buf, name = target(u, i)
        out = buf[:, lo - 512 * i:hi - 512 * i]
        bank = LIFT_BANKS[h][i]
        sem = ("pb", "pc")[i] + str(h)
        key = (sem, u)
        if lo >= plain(u):
            grp[key] = tt(sem, out, T["kg%d" % h][:, lo:hi], ps[bank][:, lo - 512 * i:hi - 512 * i], A.mult,
                          reads=["kg%d" % h, "ap%d" % bank], writes=[name], bank=[bank], tok=grp.get(key))
        elif u == 16:
            grp[key] = tt(sem, out, t[0].indirect(T.v16[:, 64 * u + lo // 16:64 * u + hi // 16]), T.kg0[:, lo:hi], A.mult,
                          reads=t[3][0] + ["v16.%d" % u, "kg0"], writes=[name], tok=grp.get(key))
        else:
            grp[key] = tt(sem, out, t[2].indirect(T.e16[:, 64 * u + lo // 16:64 * u + hi // 16]), T["am%d" % h][:, lo:hi], A.mult,
                          reads=t[3][2] + ["e16.%d" % u] + am_keys(u, lo, hi), writes=[name], tok=grp.get(key))

    def coefficients(u):
        h = u % 2
        t = tables(u)
        lo = plain(u)
        if lo < 1024:
            op("s", "kc%d" % h,
               lambda: S.activation(T["kg%d" % h][:, lo:1024], t[2].indirect(T.e16[:, 64 * u + lo // 16:64 * u + 64]), AF.Copy),
               reads=t[3][2] + ["e16.%d" % u], writes=["kg%d" % h])

    def lift(u):
        h = u % 2
        for i in range(2):
            lo, hi = max(plain(u), 512 * i), 512 * i + 512
            if lo < hi:
                bank = LIFT_BANKS[h][i]
                mms("ap%d" % i, [(ps[bank][:, lo - 512 * i:512], T.idb[:], T["am%d" % h][:, lo:hi], True, True)],
                    reads=["idb"] + am_keys(u, lo, hi), writes=["ap%d" % bank], bank=[bank])

    def loss(u):
        h = u % 2
        mms("d%d" % h, [(ps[4 + h][:, 0:64], T.qq[:, 15 - r:143 - r], T["pa%d" % h][:, r:1024:16], r == 0, r == 15) for r in range(16)],
            reads=["qq", "pa%d" % h], writes=["d%d" % h], bank=[4 + h])

    def addl(u):
        h = u % 2
        op("t", "l%d" % h, lambda: PE.matmul(ps[2 * h][:], T.idf[:], T["pb%d" % h][:], u < 2, u >= 30),
           reads=["idf", "pb%d" % h], writes=["L%d" % h], bank=[2 * h])

    def addl_dma(u):
        if u >= 2:
            op("g", "dl%d" % (u % 4), lambda: g.dma_start(T["lsb%d" % (u % 2)][:], T["pq%d" % (u % 4)][:], accum_op=A.add),
               reads=["pq%d" % (u % 4)], writes=["lsb%d" % (u % 2)], inc=16)

    def energy(u):
        h, b = u % 2, u // 16
        cb = slice(128 * b + 64 * h, 128 * b + 64 * h + 64)
        kE = "E%d%d" % (b, h)
        tt("en%d" % h, T.le[:, cb], T.le[:, cb], ps[4 + h][:, 0:64], A.subtract, reads=["le%d" % b, kE, "d%d" % h], writes=[kE], bank=[4 + h])

    def level(u, k):
        h, b = u % 2, u // 16
        H = str(h)
        c = slice(64 * h, 64 * h + 64)
        cb = slice(128 * b + 64 * h, 128 * b + 64 * h + 64)
        P = ps[4 + h]
        bk = [4 + h]
        d, m, mx, my = P[:, 0:64], P[:, 128:192], P[:, 192:256], P[:, 256:320]
        kE, kx, ky = "E%d%d" % (b, h), "x%d%d" % (b, h), "y%d%d" % (b, h)
        if k == 1:
            ts("c1" + H, T.c1[:, c], d, -0.005, A.mult, 5.4975, A.add, reads=["d" + H], writes=["c1" + H], bank=bk)
            energy(u)
        if k == 2:
            ts("m" + H, m, T.c1[:, c], 0.5, A.max, 2.0, A.min, reads=["c1" + H], writes=["m" + H], bank=bk)
            ts("e16" + H, T.e16[:, 64 * (u + 2):64 * (u + 2) + 64], T.le[:, cb], 0.015625, A.mult, -0.4921875, A.add, reads=[kE], writes=["e16.%d" % (u + 2)])
        if k == 3:
            tt("mx" + H, mx, T.dx2[:, cb], m, A.mult, reads=["dx2%d" % b, "m" + H], writes=["mx" + H], bank=bk)
            tt("my" + H, my, T.dy8[:, cb], m, A.mult, reads=["dy8%d" % b, "m" + H], writes=["my" + H], bank=bk)
        if k == 4:
            tt("x" + H, T.lx[:, cb], T.lx[:, cb], mx, A.add, reads=["lx%d" % b, "v16.%d" % u, kx, "mx" + H], writes=[kx], bank=bk)
            tt("y" + H, T.y4[:, cb], T.y4[:, cb], my, A.add, reads=["y4%d" % b, "v16.%d" % u, ky, "my" + H], writes=[ky], bank=bk)
        if k == 5:
            ts("vx" + H, T.vxb[:, c], T.lx[:, cb], 1023, A.bitwise_and, 4, A.arith_shift_right, reads=[kx], writes=["vxb" + H])
            ts("vy" + H, T.vyb[:, c], T.y4[:, cb], 0xFC0, A.bitwise_and, reads=[ky], writes=["vyb" + H])
        if k == 6:
            tt("v" + H, T.vb[:, c], T.vxb[:, c], T.vyb[:, c], A.add, reads=["vxb" + H, "vyb" + H], writes=["vb" + H])
            if u in (12, 13):
                tt("c2" + H, T.ef[:, c], T.le[:, cb], T.lf[:, c], A.subtract, reads=[kE, "lf"], writes=["ef" + H])
        if k == 7:
            cp("v16" + H, T.v16[:, 64 * (u + 2):64 * (u + 2) + 64], T.vb[:, c], reads=["vb" + H], writes=["v16.%d" % (u + 2)])
            if u < 14 and (u // 2) % 2 == 0:
                for kk in range(2):
                    o = 256 * (u // 4) + 128 * h + 64 * kk
                    ts(("ka", "kb")[kk] + H, T.mk[:, o:o + 64], T.vb[:, c], 2048.0, (A.is_lt, A.is_ge)[kk],
                       reads=["vb" + H], writes=["mk%d%d%d" % (u // 4, h, kk)])

    def verdict(h, k):
        H = str(h)
        c = slice(64 * h, 64 * h + 64)
        P = ps[4 + h]
        bk = [4 + h]
        d, z, t = P[:, 0:64], P[:, 320:384], P[:, 384:448]
        if k == 1:
            tt("c1" + H, T.df[:, c], T.ef[:, c], d, A.subtract, reads=["ef" + H, "d" + H], writes=["df" + H], bank=bk)
            energy(14 + h)
        if k == 2:
            ts("m" + H, T.df[:, c], T.df[:, c], -1.0, A.max, 1.0, A.min, reads=["df" + H], writes=["df" + H])
        if k == 3:
            tt("mx" + H, T.sb[:, c], T.df[:, c], T.lo[:, c], A.max, reads=["df" + H, "lo"], writes=["sb" + H])
            mms("uz" + H, [(z, T.cm[:], T.sb[:, c], True, True)], reads=["cm", "sb" + H], writes=["z" + H], bank=bk)
        if k == 4:
            ts("x" + H, t, z, -1.0, A.max, 1.0, A.min, reads=["z" + H], writes=["t" + H], bank=bk)
        if k >= 5:
            j = k - 5
            out = T["uout%d" % j] if j else T.uin0
            tok = None
            for kk in range(2):
                o = 128 * h + 64 * kk
                tok = tt(("vx", "vy", "v", "v16")[j] + H, out[:, o:o + 64], T.mk[:, 256 * j + o:256 * j + o + 64], t, A.mult,
                         reads=["t" + H, "mk%d%d%d" % (j, h, kk)], writes=["u%d%d" % (j, h)], bank=bk, tok=tok)
            if j:
                need("g", deps("g", ["u%d%d" % (j, h)], (), ()))
                o = slice(128 * h, 128 * h + 128)
                sent[0] += send(g, T, topo, core, T.cores[(rank + j) % N], T["uin%d" % j][:, o], out[:, o], "ua" + H)

    def exit_energy(u, k):
        c = slice(128 * (u // 16) + 64 * (u % 2), 128 * (u // 16) + 64 * (u % 2) + 64)
        ch = slice(64 * (u % 2), 64 * (u % 2) + 64)
        H = str(u % 2)
        if k == 2:
            ts("c2" + H, T.vxb[:, ch], T.le[:, c], 0.0, A.max, reads=["E%d%s" % (u // 16, H)], writes=["vxb" + H])
        if k == 3:
            ts("ka" + H, T.vyb[:, ch], T.vxb[:, ch], 1023, A.bitwise_and, reads=["vxb" + H], writes=["vyb" + H])
        if k == 4:
            cp("kb" + H, T.yeb[:, c], T.vyb[:, ch], reads=["vyb" + H], writes=["yeb%d" % u])

    def follow(u, k):
        if u in (14, 15):
            for kk in {5: (6, 7), 6: (8,), 7: (5,)}.get(k, (k,)):
                verdict(u % 2, kk)
        elif u < 30:
            level(u, k)
        elif k == 1:
            energy(u)
        if u % 16 >= 14:
            exit_energy(u, k)

    def ahead(u, i):
        t = tables(u)
        w, c = 1 + i // 4, slice(256 * (i % 4), 256 * (i % 4) + 256)
        name = ("am0", "kg0")[w - 1]
        grp[name] = op("s", ("sa", "sk")[w - 1], lambda: S.activation(T[name][:, c], t[w].indirect(T.e16[:, 64 * u + 16 * (i % 4):64 * u + 16 * (i % 4) + 16]), AF.Copy),
                       reads=t[3][w] + ["e16.%d" % u], writes=am_keys(u, 0, 1024) if w == 1 else ["kg0"], tok=grp.get(name))

    def start(u):
        if u == 0:
            amounts(u)
        amounts(u + 1)
        coefficients(u + 1)

    def unit(u):
        for x in SLOT:
            if x[0] == "loss":
                losses(u, x[1], x[2])
                if x[2] == 1024:
                    loss(u)
                    if u % 16:
                        addl(u - 1)
            elif x[0] == "dose":
                doses(u, x[1], x[2])
            elif x[0] == "new":
                follow(u, x[1])
            elif u % 16:
                follow(u - 1, x[1])
                if x[1] == 7 and u % 16 < 15:
                    amounts(u + 1)
                    if u + 1 in FRESH:
                        coefficients(u + 1)
                if x[1] == 7 and u == 15:
                    addl_dma(14)
            elif u == 0 and x[1] == 7:
                strides(0)
        if u == 3:
            load_late("v16.4")
        if u == 8:
            ts("vc", T.lo[:], T.lf[:], 0.0, A.is_gt, -1.0, A.mult, reads=["lf"], writes=["lo"])
        if u % 16 < 15:
            lift(u + 1)
        if u % 16 < 14 and u + 2 not in FRESH:
            coefficients(u + 2)
        side(u)
        if u < 30 and u not in (14, 15):
            addl_dma(u)

    scatter(0, EARLY)
    start(0)
    for u in range(16):
        unit(u)
    exit_energy(15, 4)
    steps = offsets(1)
    next(steps)
    verdict(1, 4)
    strides(1)
    for k in (6, 7, 8, 5):
        verdict(1, k)
    for _ in steps:
        pass
    addl_dma(15)
    grp["st"] = op("y", "st", lambda: g.sync.dma_start(T.ye[:, 0:128], T.yeb[:, 0:128]), reads=["yeb14", "yeb15"], inc=16)

    uin = [T["uin%d" % j] for j in range(4)]
    ub, xb = (4, 5, 1), (3, 6)

    def prefix(h):
        tok = None
        for j in range(4):
            tok = mms("n%d" % h, [(ps[6 + h][:, j:512:4], T.idn[:], uin[i][:, 128 * h:128 * h + 128], i == 0, i == j) for i in range(j + 1)],
                      reads=["idn", "u0%d" % h] + (["uin%d" % h] if j else []), writes=["n%d" % h], bank=[6 + h], tok=tok)

    def bounds(h):
        c = slice(512 * h, 512 * h + 512)
        o = slice(128 * h, 128 * h + 128)
        op("v", "sm%d" % h, lambda: V.tensor_tensor_scan(T.scm[:, c], T.rst[:], ps[6 + h][:], 0.0, A.mult, A.min), reads=["rst", "n%d" % h], writes=["scm%d" % h], bank=[6 + h])
        op("v", "sz%d" % h, lambda: V.tensor_tensor_scan(T.scz[:, c], T.rst[:], ps[6 + h][:], 0.0, A.mult, A.max), reads=["rst", "n%d" % h], writes=["scz%d" % h], bank=[6 + h])
        ts("vd", T.uu[:, o], T.scm[:, 512 * h + 3:512 * h + 512:4], 15.0, A.add, reads=["scm%d" % h], writes=["uu%d" % h])
        ts("tc%d" % h, T.tt[:, o], ps[6 + h][:, 3:512:4], -1.0, A.mult, reads=["n%d" % h], writes=["tt%d" % h], bank=[6 + h])

    def row(i, par):
        r = i % 8 + 8 * par
        return T.wp[:, 128 * r:128 * r + 128]

    def spread(i):
        h, k = i // 8, i % 3
        tok = None
        for o, src, key in ((256, T.scz[:, 512 * h + 3:512 * h + 512:4], "scz%d" % h), (0, T.uu[:, 128 * h:128 * h + 128], "uu%d" % h)):
            for par in range(2):
                tok = mms("uz%d" % k, [(ps[ub[k]][:, o + par:o + 256:2], row(i, par), src, True, True)], reads=["wp", key], writes=["U%d" % k], bank=[ub[k]], tok=tok)

    prefix(0)
    bounds(0)
    for i in range(3):
        spread(i)
    for i in range(16):
        h, k, x = i // 8, i % 3, i % 2
        K = str(k)
        a = T.acor[:, 2048 * h + i % 8:2048 * h + 2048:8]
        tt("mm" + K, T["mb" + K][:], a, ps[ub[k]][:, 256:512], A.is_gt, reads=["acor%d" % h, "U" + K], writes=["mb" + K], bank=[ub[k]])
        tt("g" + K, T["gb" + K][:], a, ps[ub[k]][:, 0:256], A.min, reads=["acor%d" % h, "U" + K], writes=["gb" + K], bank=[ub[k]])
        if i == SECOND[1]:
            bounds(1)
        X = ps[xb[x]]
        mms("xx%d" % x, [(X[:, 0:256], T.id32[:], T["mb" + K][:], True, False), (X[:, 0:256:2], row(i, 0), T.tt[:, 128 * h:128 * h + 128], False, False),
                         (X[:, 1:256:2], row(i, 1), T.tt[:, 128 * h:128 * h + 128], False, False), (X[:, 0:256], T.idb[:], T["gb" + K][:], False, True)],
            reads=["wp", "tt%d" % h, "idb", "id32", "gb" + K, "mb" + K], writes=["X%d" % x], bank=[xb[x]])
        if i == SECOND[0]:
            prefix(1)
        if i + 3 < 16:
            spread(i + 3)
        op("s", "f%d" % x, lambda: S.activation(T.fn[:, 256 * i:256 * i + 256], X[:, 0:256], AF.Relu, bias=-32.0), reads=["X%d" % x], writes=["fn%d" % i], bank=[xb[x]])
        if i < LATE[1] // 128:
            scatter(4096 - LATE[1] + 128 * i, 4096 - LATE[1] + 128 * i + 128)
        if i == LATE[1] // 128 - 1:
            inverse()
        if 5 <= i < 13:
            ahead(16, i - 5)
        if i == 14:
            cp("vd", T.invi[:], T.invl[:], reads=["invl"], writes=["invi"])
    ts("ve", T.inv16[:], T.invi[:], -512.0, A.add, reads=["invi"], writes=["inv16"])
    addl(15)
    fn = ["fn%d" % r for r in range(16)]
    order = (0, 2, 1, 3, 4, 6, 5, 7)
    for p in order:
        out = T.slb0[:, 512 * p:512 * p + 512]
        src = T.fn[:, 0:4096].indirect(T.inv16[:, 32 * p:32 * p + 32])
        if p % 4 < 2:
            cp("pm%d" % p, out, src, reads=fn + ["inv16"], writes=["slb0.%d" % p])
        else:
            op("s", "pm%d" % p, lambda: S.activation(out, src, AF.Copy), reads=fn + ["inv16"], writes=["slb0.%d" % p])
    hand_out_slab(order)

    def finish(h, i):
        k = 2 * h + i
        if i:
            bank = LIFT_BANKS[h][1]
            tt("mx%d" % h, T["lsb%d" % h][:], T["lsb%d" % h][:], ps[bank][:], A.add, reads=["lsb%d" % h, "ap%d" % bank], writes=["lsb%d" % h], bank=[bank])
        src = T["lsb%d" % h] if i else ps[2 * h]
        op("s", "ex%d" % i, lambda: S.activation(T.ylb[:, 512 * k:512 * k + 512], src[:], AF.Exp, scale=-0.0078125),
           reads=["lsb%d" % h if i else "L%d" % h], writes=["ylb%d" % k], bank=[] if i else [2 * h])
        grp["st"] = op("y", "st", lambda: g.sync.dma_start(T.yl[:, 512 * k:512 * k + 512], T.ylb[:, 512 * k:512 * k + 512]),
                       reads=["ylb%d" % k], inc=16, tok=grp.get("st"))

    start(16)
    for u in range(16, 31):
        unit(u)
    addl(30)
    finish(0, 1)
    follow(30, 4)
    doses(31, 0, 512)
    addl(31)
    finish(0, 0)
    finish(1, 0)
    for lo, hi in chunks:
        losses(31, lo, hi)
    loss(31)
    doses(31, 512, 1024)
    follow(31, 1)
    finish(1, 1)
    for k in (2, 3, 4):
        follow(31, k)
    op("y", "st", lambda: g.sync.dma_start(T.ye[:, 128:256], T.yeb[:, 128:256]), reads=["yeb30", "yeb31"], inc=16, tok=grp["st"])

    g.wait_ge(T.sem.ls, sent[0])
    for s, n in cnt.items():
        if max(know[q].get(s, 0) for q in Q) < n:
            g.wait_ge(T.sem[s], n)
